import numpy as np
import ml_dtypes


def mxq(x, axis, fmt="e4m3"):
    dtype, down = {"e4m3": (ml_dtypes.float8_e4m3fn, 7), "e5m2": (ml_dtypes.float8_e5m2, 14)}[fmt]
    v = np.moveaxis(np.asarray(x, np.float32).astype(ml_dtypes.bfloat16).astype(np.float64), axis, -1)
    blocks = v.reshape(v.shape[:-1] + (-1, 32))
    amax = np.abs(blocks).max(-1, keepdims=True)
    byte = np.maximum(np.where(amax > 0, np.frexp(amax)[1] - 1 + 127, 0) - down, 1)
    scale = np.exp2(byte - 127.0)
    codes = (blocks / scale).astype(np.float32).astype(dtype).astype(np.float64)
    return np.moveaxis((codes * scale).reshape(v.shape), -1, axis)


WIDE = False


def mx_kscale(k):
    if not WIDE:
        return np.ones(k)
    levels = np.array([10, -10, 5, -5, 0])
    if k % 512:
        return np.exp2(np.random.permutation(np.resize(levels, k // 32))).repeat(32)
    a = np.empty((k // 512, 16))
    for p in range(k // 512):
        a[p, :8] = np.random.permutation(np.resize(levels, 8))
        for g in range(8):
            far = levels[np.abs(levels - a[p, g]) >= 10]
            a[p, g + 8] = far[np.random.randint(len(far))]
    return np.exp2(a.ravel()).repeat(32)


BF16 = ml_dtypes.bfloat16


def bf(x):
    return np.asarray(x, np.float32).astype(BF16)


def f64(x):
    return np.asarray(x).astype(np.float64)


N, D, H, O = 1024, 1024, 1024, 512
DAMP = 0.2


def draw0():
    u = mx_kscale(O)
    t = mx_kscale(N)
    return {
        "x": bf(np.random.standard_normal((N, D))),
        "a": bf(np.random.standard_normal((N, H))),
        "g": bf(np.random.standard_normal((N, O)) * u[None, :]),
        "w2": bf(np.random.standard_normal((H, O)) / np.sqrt(O) / u[None, :]),
        "p": bf(np.random.uniform(0.5, 1.5, N) * t),
        "q": bf(np.random.uniform(0.5, 1.5, N) / t),
        "s": bf(np.random.standard_normal(N)),
    }


def backprop_delta(a, g, w2):
    back = mxq(g, 1, "e4m3") @ mxq(w2, 1, "e4m3").T
    return back * (1.0 - np.tanh(a) ** 2)


def core(x, a, g, w2, p, q, s):
    x, a, g, w2, p, q, s = f64(x), f64(a), f64(g), f64(w2), f64(p), f64(q), f64(s)
    n = x.shape[0]

    d = backprop_delta(a, g, w2)

    xp = x * p[:, None]
    dq = d * q[:, None]
    grad = (mxq(xp, 0, "e4m3").T @ mxq(dq, 0, "e4m3")) / np.sqrt(n)

    x2 = x * xp * s[:, None]
    d2 = d * dq * s[:, None]
    fisher = (mxq(x2, 0, "e4m3").T @ mxq(d2, 0, "e4m3")) / n

    return grad / (fisher + DAMP)


def e4m3fn_bytes(y):
    return np.clip(np.asarray(y, np.float64), -448.0, 448.0).astype(np.float32).astype(ml_dtypes.float8_e4m3fn).view(np.uint8)


def e4m3fn_values(b):
    return np.asarray(b, np.uint8).view(ml_dtypes.float8_e4m3fn).astype(np.float64)


def setup_inputs():
    d = draw0()
    x0 = np.asarray(d['w2']).astype(np.float64)
    s = (np.max(np.abs(x0), axis=(0,), keepdims=True) / 448.0).astype(np.float32)
    out = {}
    for k, v in d.items():
        if k == 'w2':
            out['w2_bytes'] = e4m3fn_bytes(x0 / s.astype(np.float64))
            out['w2_scale'] = s
        else:
            out[k] = v
    return out


def reference(x, a, g, w2_bytes, w2_scale, p, q, s):
    return core(x, a, g, e4m3fn_values(w2_bytes) * w2_scale.astype(np.float64), p, q, s)

@@ -1,0 +1,328 @@
+from contextlib import ExitStack
+
+import concourse.mybir as mybir
+from concourse.masks import make_identity
+
+N, D, H, O = 1024, 1024, 1024, 512
+FLOPS = 2 * N * H * O + 2 * 2 * N * D * H
+
+F32 = mybir.dt.float32
+BF16 = mybir.dt.bfloat16
+U32 = mybir.dt.uint32
+U8 = mybir.dt.uint8
+FP8 = mybir.dt.float8_e4m3fn
+FP8X4 = mybir.dt.float8_e4m3fn_x4
+ALU = mybir.AluOpType
+ACT = mybir.ActivationFunctionType
+
+P = 128
+T = 4
+G = 2
+HH = 512
+DC = 128
+
+
+def tile_diagonalfishernaturalgradient_kernel(tc, x, a, g, w2_bytes, w2_scale, p, q, s, out):
+    nc = tc.nc
+    with ExitStack() as ctx:
+        keep = ctx.enter_context(tc.tile_pool(name="keep", bufs=1))
+        stage = ctx.enter_context(tc.tile_pool(name="stage", bufs=2))
+        psa = ctx.enter_context(tc.psum_pool(name="psa", bufs=8))
+
+        pqs_raw = [keep.tile([P, G * T], BF16, name="raw_%d" % i) for i in range(3)]
+        for i, v in enumerate((s, p, q)):
+            nc.scalar.dma_start(out=pqs_raw[i][:].rearrange("p (g t) -> p g t", t=T), in_=v.rearrange("(g p t) -> p g t", p=P, t=T))
+        w_scale = keep.tile([P, T], F32, name="w_scale")
+        nc.scalar.dma_start(out=w_scale[:], in_=w2_scale.rearrange("o (p t) -> p (o t)", t=T))
+        w_raw = keep.tile([P, 8 * O], U8, name="w_raw")
+        w_view = w2_bytes.rearrange("(r p) k -> p r k", p=P)
+
+        def load_w(i):
+            nc.sync.dma_start(out=w_raw[:, i * 2048:(i + 1) * 2048].rearrange("p (r k) -> p r k", k=O), in_=w_view[:, 4 * i:4 * i + 4, :])
+
+        g_raw = [keep.tile([P, T, O], BF16, name="g_raw%d" % i) for i in range(G)]
+        a_raw = [keep.tile([P, T, H], BF16, name="a_raw%d" % i) for i in range(G)]
+        x_raw = [keep.tile([P, T, D], BF16, name="x_raw%d" % i) for i in range(G)]
+        g_view = g.rearrange("(g p t) k -> g p t k", p=P, t=T)
+        a_view = a.rearrange("(g p t) k -> g p t k", p=P, t=T)
+        x_view = x.rearrange("(g p t) k -> g p t k", p=P, t=T)
+        load_w(0)
+        load_w(1)
+        nc.sync.dma_start(out=a_raw[0][:, :, 0:512], in_=a_view[0][:, :, 0:512])
+        nc.sync.dma_start(out=g_raw[0][:], in_=g_view[0])
+        nc.sync.dma_start(out=x_raw[0][:, :, 0:512], in_=x_view[0][:, :, 0:512])
+        nc.sync.dma_start(out=a_raw[1][:], in_=a_view[1])
+        nc.sync.dma_start(out=g_raw[1][:], in_=g_view[1])
+        nc.sync.dma_start(out=x_raw[1][:], in_=x_view[1])
+        nc.sync.dma_start(out=a_raw[0][:, :, 512:1024], in_=a_view[0][:, :, 512:1024])
+        nc.sync.dma_start(out=x_raw[0][:, :, 512:1024], in_=x_view[0][:, :, 512:1024])
+        warm = keep.tile([P, 1], F32, name="warm")
+        nc.vector.memset(warm[:], 0.0)
+        nc.scalar.activation(out=warm[:], in_=warm[:], func=ACT.Tanh)
+
+        ident = keep.tile([P, P], F32, name="ident")
+        make_identity(nc, ident[:])
+
+        quarter = keep.tile([P, 2 * G * T], F32, name="quarter")
+        nc.gpsimd.memset(quarter[:], 0.25)
+        pqs = keep.tile([P, 3, G * T], F32, name="pqs")
+        for i, j in ((2, 0), (0, 1), (1, 2)):
+            nc.vector.tensor_copy(out=pqs[:, i, :], in_=pqs_raw[j][:])
+        weight = keep.tile([P, 2, G * T], F32, name="weight")
+        nc.vector.tensor_tensor(out=weight[:], in0=pqs[:, 0:2, :], in1=pqs[:, 2:3, :].to_broadcast([P, 2, G * T]), op=ALU.mult)
+        magnitude = keep.tile([P, 2, G * T], F32, name="magnitude")
+        nc.vector.scalar_tensor_tensor(out=magnitude[:], in0=weight[:], scalar=-1.0, in1=weight[:], op0=ALU.mult, op1=ALU.max)
+        nc.vector.tensor_scalar(out=magnitude[:], in0=magnitude[:], scalar1=2.0 ** -100, scalar2=None, op0=ALU.max)
+        root4 = keep.tile([P, 2, G * T], F32, name="root4")
+        nc.gpsimd.tensor_tensor(out=root4[:].rearrange("p a j -> p (a j)"), in0=magnitude[:].rearrange("p a j -> p (a j)"), in1=quarter[:], op=ALU.pow)
+        root2 = keep.tile([P, 2, G * T], F32, name="root2")
+        nc.vector.tensor_tensor(out=root2[:], in0=root4[:], in1=root4[:], op=ALU.mult)
+        f_inv = keep.tile([P, G * T], F32, name="f_inv")
+        nc.vector.reciprocal(out=f_inv[:], in_=root2[:, 1, :])
+        neg_c = keep.tile([P, G * T], F32, name="neg_c")
+        nc.vector.scalar_tensor_tensor(out=neg_c[:], in0=f_inv[:], scalar=-1.0, in1=pqs[:, 1, :], op0=ALU.mult, op1=ALU.mult)
+        r_hi = keep.tile([P, G * T], BF16, name="r_hi")
+        nc.vector.tensor_copy(out=r_hi[:], in_=root2[:, 0, :])
+        r_lo = keep.tile([P, G * T], F32, name="r_lo")
+        nc.vector.tensor_tensor(out=r_lo[:], in0=root2[:, 0, :], in1=r_hi[:], op=ALU.subtract)
+        diag = keep.tile([P, 2, G * T, P], BF16, name="diag")
+        for i, r in enumerate((r_hi, r_lo)):
+            nc.gpsimd.tensor_tensor(out=diag[:, i], in0=ident[:].unsqueeze(1).to_broadcast([P, G * T, P]), in1=r[:].unsqueeze(2).to_broadcast([P, G * T, P]), op=ALU.mult)
+
+        w_wide = keep.tile([P, 8 * O], BF16, name="w_wide")
+        w_codes = keep.tile([P, H], U32, name="w_codes", align_bytes=64)
+        w_scales = keep.tile([P, H], U8, name="w_scales", align_bytes=64)
+        scale_pair = w_scale[:].rearrange("p (u e) -> p u e", e=2).unsqueeze(1).to_broadcast([P, 256, 2, 2])
+        w_il = {}
+
+        def cast_w(hh):
+            half = slice(hh * 2048, (hh + 1) * 2048)
+            nc.scalar.copy(out=w_wide[:, half], in_=w_raw[:, half].bitcast(FP8))
+
+        def turn_w(hh, b):
+            if b == 0:
+                w_il[hh] = stage.tile([P, HH, T], BF16, name="w_il", align_bytes=64)
+            bank = psa.tile([P, 512], F32, name="psa")
+            for rr in range(2):
+                r = 4 * hh + 2 * b + rr
+                words = w_wide[:, r * O:(r + 1) * O].bitcast(F32)
+                for u in range(2):
+                    nc.tensor.transpose(bank[:, u * 256 + rr * P:u * 256 + (rr + 1) * P], words[:, u::2], ident[:])
+            nc.vector.tensor_tensor(
+                out=w_il[hh][:, b * 256:(b + 1) * 256, :].rearrange("p h (u e) -> p h u e", e=2),
+                in0=bank[:].bitcast(BF16).rearrange("p (u h e) -> p h u e", u=2, e=2),
+                in1=scale_pair, op=ALU.mult)
+
+        def quant_w(hh):
+            cols = slice(hh * HH, (hh + 1) * HH)
+            nc.vector.quantize_mx(out=w_codes[:, cols].bitcast(FP8X4), scales=w_scales[:, cols], in_=w_il[hh][:].rearrange("p h t -> p (h t)"))
+
+        g_codes = keep.tile([P, G, 512], U32, name="g_codes", align_bytes=64)
+        g_scales = keep.tile([P, G, 512], U8, name="g_scales", align_bytes=64)
+
+        g_ils = {}
+
+        def turn_g(i):
+            g_il = stage.tile([P, T * P, T], BF16, name="g_il", align_bytes=64)
+            g_ils[i] = g_il
+            for b in range(2):
+                bank = psa.tile([P, 512], F32, name="psa")
+                for tt in range(2):
+                    words = g_raw[i][:, 2 * b + tt, :].bitcast(F32)
+                    for u in range(2):
+                        nc.tensor.transpose(bank[:, (2 * tt + u) * P:(2 * tt + u + 1) * P], words[:, u::2], ident[:])
+                nc.scalar.copy(
+                    out=g_il[:, b * 256:(b + 1) * 256, :].rearrange("p n t -> p (n t)").bitcast(F32).rearrange("p (t m u) -> p t m u", t=2, u=2),
+                    in_=bank[:].rearrange("p (t u m) -> p t m u", t=2, u=2))
+
+        def quant_g(i):
+            nc.vector.quantize_mx(out=g_codes[:, i, :].bitcast(FP8X4), scales=g_scales[:, i, :], in_=g_ils[i][:].rearrange("p n t -> p (n t)"))
+
+        xp_codes = keep.tile([P, G, D], U32, name="xp_codes", align_bytes=64)
+        xp_scales = keep.tile([P, G, D], U8, name="xp_scales", align_bytes=64)
+        x2_codes = keep.tile([P, G, D], U32, name="x2_codes", align_bytes=64)
+        x2_scales = keep.tile([P, G, D], U8, name="x2_scales", align_bytes=64)
+
+        xp_ils = {}
+        x2_ils = {}
+
+        def make_xp(i, half):
+            cols = slice(half * 512, half * 512 + 512)
+            planar = stage.tile([P, T, 512], BF16, name="xp_planar")
+            for t in range(T):
+                nc.vector.tensor_scalar(out=planar[:, t, :], in0=x_raw[i][:, t, cols], scalar1=pqs[:, 0, i * T + t:i * T + t + 1], scalar2=None, op0=ALU.mult)
+            il = stage.tile([P, 512, T], BF16, name="xp_il", align_bytes=64)
+            xp_ils[i, half] = il
+            nc.vector.tensor_copy(out=il[:], in_=planar[:].rearrange("p t d -> p d t"))
+
+        def quant_xp(i, half):
+            cols = slice(half * 512, half * 512 + 512)
+            il = xp_ils[i, half]
+            nc.vector.quantize_mx(out=xp_codes[:, i, cols].bitcast(FP8X4), scales=xp_scales[:, i, cols], in_=il[:].rearrange("p d t -> p (d t)"))
+
+        def make_x2(i, half):
+            il = stage.tile([P, 512, T], BF16, name="x2_il", align_bytes=64)
+            x2_ils[i, half] = il
+            for b in range(4):
+                bank = psa.tile([P, 512], F32, name="psa")
+                for t in range(T):
+                    cols = slice(half * 512 + b * DC, half * 512 + (b + 1) * DC)
+                    for k in range(2):
+                        nc.tensor.matmul(bank[:, t * DC:(t + 1) * DC], lhsT=diag[:, k, i * T + t, :], rhs=x_raw[i][:, t, cols], start=(k == 0), stop=(k == 1))
+                nc.scalar.activation(out=il[:, b * DC:(b + 1) * DC, :], in_=bank[:].rearrange("p (t d) -> p d t", t=T), func=ACT.Square)
+
+        def quant_x2(i, half):
+            cols = slice(half * 512, half * 512 + 512)
+            il = x2_ils[i, half]
+            nc.vector.quantize_mx(out=x2_codes[:, i, cols].bitcast(FP8X4), scales=x2_scales[:, i, cols], in_=il[:].rearrange("p d t -> p (d t)"))
+
+        dq_codes = keep.tile([P, G, H], U32, name="dq_codes", align_bytes=64)
+        dq_scales = keep.tile([P, G, H], U8, name="dq_scales", align_bytes=64)
+        d2_codes = keep.tile([P, G, H], U32, name="d2_codes", align_bytes=64)
+        d2_scales = keep.tile([P, G, H], U8, name="d2_scales", align_bytes=64)
+        th = {}
+
+        def make_tanh(i, hh):
+            th[i, hh] = keep.tile([P, T, HH], F32, name="th%d%d" % (i, hh))
+            nc.scalar.activation(out=th[i, hh][:], in_=a_raw[i][:, :, hh * HH:(hh + 1) * HH], func=ACT.Tanh)
+
+        def make_sech(i, hh):
+            for t in range(T):
+                j = i * T + t
+                nc.scalar.activation(out=th[i, hh][:, t, :], in_=th[i, hh][:, t, :], func=ACT.Square, scale=root4[:, 1, j:j + 1])
+
+        def make_e(i, hh, t):
+            j = i * T + t
+            bank = psa.tile([P, 512], F32, name="psa")
+            nc.tensor.matmul_mx(
+                out=bank[:], lhsT=g_codes[:, i, t * P:(t + 1) * P].bitcast(FP8X4), lhsT_scale=g_scales[:, i, t * P:(t + 1) * P],
+                rhs=w_codes[:, hh * HH:(hh + 1) * HH].bitcast(FP8X4), rhs_scale=w_scales[:, hh * HH:(hh + 1) * HH], start=True, stop=True)
+            nc.vector.scalar_tensor_tensor(out=th[i, hh][:, t, :], in0=th[i, hh][:, t, :], scalar=root2[:, 1, j:j + 1], in1=bank[:], op0=ALU.subtract, op1=ALU.mult)
+
+        d_ils = {}
+
+        def make_d(i, c0, w):
+            hh, off = divmod(c0, HH)
+            e = th[i, hh][:, :, off:off + w].rearrange("p t h -> p h t")
+            d2_il = stage.tile([P, w, T], BF16, name="d2_il", align_bytes=64)
+            dq_il = stage.tile([P, w, T], BF16, name="dq_il", align_bytes=64)
+            d_ils[i, c0] = (dq_il, d2_il)
+            nc.scalar.activation(out=d2_il[:], in_=e, func=ACT.Square)
+            nc.vector.tensor_tensor(out=dq_il[:], in0=e, in1=neg_c[:, i * T:(i + 1) * T].unsqueeze(1).to_broadcast([P, w, T]), op=ALU.mult)
+
+        def quant_d(i, c0, w):
+            cols = slice(c0, c0 + w)
+            dq_il, d2_il = d_ils[i, c0]
+            nc.vector.quantize_mx(out=d2_codes[:, i, cols].bitcast(FP8X4), scales=d2_scales[:, i, cols], in_=d2_il[:].rearrange("p h t -> p (h t)"))
+            nc.vector.quantize_mx(out=dq_codes[:, i, cols].bitcast(FP8X4), scales=dq_scales[:, i, cols], in_=dq_il[:].rearrange("p h t -> p (h t)"))
+
+        live = {}
+
+        def product(m, c0, w, lc, ls, rc, rs):
+            cols = slice(c0, c0 + w)
+            bank = psa.tile([P, 512], F32, name="psa")
+            for b in range(512 // w):
+                rows = slice((m + b) * P, (m + b + 1) * P)
+                for i in range(G):
+                    nc.tensor.matmul_mx(out=bank[:, b * w:(b + 1) * w], lhsT=lc[:, i, rows].bitcast(FP8X4), lhsT_scale=ls[:, i, rows], rhs=rc[:, i, cols].bitcast(FP8X4), rhs_scale=rs[:, i, cols], start=(i == 0), stop=(i == G - 1))
+            return bank
+
+        def open_tile(m, c0, w):
+            fish = product(m, c0, w, x2_codes, x2_scales, d2_codes, d2_scales)
+            inv_root = stage.tile([P, 512], F32, name="inv_root", bufs=3)
+            nc.scalar.activation(out=inv_root[:], in_=fish[:], func=ACT.Abs_reciprocal_sqrt, scale=1.0 / 32.0, bias=6.4)
+            live[m, c0] = inv_root
+
+        def close_tile(m, c0, w, on_vector):
+            grad = product(m, c0, w, xp_codes, xp_scales, dq_codes, dq_scales)
+            inv_root = live[m, c0]
+            res = stage.tile([P, 512], F32, name="res", bufs=4)
+            if on_vector:
+                part = stage.tile([P, 512], F32, name="part")
+                nc.vector.tensor_tensor(out=part[:], in0=grad[:], in1=inv_root[:], op=ALU.mult)
+                nc.vector.tensor_tensor(out=res[:], in0=part[:], in1=inv_root[:], op=ALU.mult)
+            else:
+                inv = stage.tile([P, 512], F32, name="inv")
+                nc.scalar.activation(out=inv[:], in_=inv_root[:], func=ACT.Square)
+                nc.vector.tensor_tensor(out=res[:], in0=grad[:], in1=inv[:], op=ALU.mult)
+            blocks = 512 // w
+            nc.sync.dma_start(
+                out=out[m * P:(m + blocks) * P, c0:c0 + w].rearrange("(b p) h -> p b h", p=P),
+                in_=res[:].rearrange("p (b h) -> p b h", b=blocks))
+
+        ctx.enter_context(tc.manual_schedule())
+        cast_w(0)
+        turn_w(0, 0)
+        cast_w(1)
+        turn_w(0, 1)
+        make_tanh(0, 0)
+        turn_w(1, 0)
+        turn_w(1, 1)
+        turn_g(0)
+        quant_w(0)
+        make_sech(0, 0)
+        make_xp(0, 0)
+        make_tanh(1, 0)
+        quant_g(0)
+        make_x2(0, 0)
+        for t in range(T):
+            make_e(0, 0, t)
+        quant_w(1)
+        quant_xp(0, 0)
+        turn_g(1)
+        make_sech(1, 0)
+        make_d(0, 0, 512)
+        quant_x2(0, 0)
+        quant_g(1)
+        for t in range(T):
+            make_e(1, 0, t)
+        make_x2(1, 0)
+        quant_d(0, 0, 512)
+        make_d(1, 0, 512)
+        make_xp(1, 0)
+        make_tanh(0, 1)
+        make_tanh(1, 1)
+        quant_x2(1, 0)
+        quant_d(1, 0, 512)
+        quant_xp(1, 0)
+        make_xp(0, 1)
+        make_xp(1, 1)
+        quant_xp(0, 1)
+        quant_xp(1, 1)
+
+        def side(k):
+            if k == 0:
+                make_x2(0, 1)
+            if k == 1:
+                make_x2(1, 1)
+                quant_x2(0, 1)
+            if k == 2:
+                make_sech(0, 1)
+                for t in range(T):
+                    make_e(0, 1, t)
+            if k == 3:
+                make_sech(1, 1)
+                quant_x2(1, 1)
+                for t in range(T):
+                    make_e(1, 1, t)
+            if k == 4:
+                make_d(0, 512, 256)
+                make_d(1, 512, 256)
+            if k == 5:
+                quant_d(0, 512, 256)
+                quant_d(1, 512, 256)
+            if k == 6:
+                make_d(0, 768, 256)
+            if k == 7:
+                make_d(1, 768, 256)
+            if k == 8:
+                quant_d(0, 768, 256)
+                quant_d(1, 768, 256)
+
+        order = [(m, 0, 512) for m in range(8)] + [(m, c0, 256) for c0 in (512, 768) for m in range(0, 8, 2)]
+        for k in range(17):
+            if k < 16:
+                open_tile(*order[k])
+            if k > 0:
+                close_tile(*order[k - 1], on_vector=(k % 2 == 0))
+            side(k)

@@ -18,8 +18,8 @@ ACT = mybir.ActivationFunctionType
 P = 128
 T = 4
 G = 2
-HH = 512
-DC = 128
+D_CHUNKS = ((0, 512), (512, 256), (768, 256))
+X_CHUNKS = ((0, 512), (512, 256), (768, 256))
 
 
 def tile_diagonalfishernaturalgradient_kernel(tc, x, a, g, w2_bytes, w2_scale, p, q, s, out):
@@ -27,47 +27,52 @@ def tile_diagonalfishernaturalgradient_kernel(tc, x, a, g, w2_bytes, w2_scale, p
     with ExitStack() as ctx:
         keep = ctx.enter_context(tc.tile_pool(name="keep", bufs=1))
         stage = ctx.enter_context(tc.tile_pool(name="stage", bufs=2))
-        psa = ctx.enter_context(tc.psum_pool(name="psa", bufs=8))
+        psum = ctx.enter_context(tc.psum_pool(name="psum", bufs=8))
 
-        pqs_raw = [keep.tile([P, G * T], BF16, name="raw_%d" % i) for i in range(3)]
-        for i, v in enumerate((s, p, q)):
-            nc.scalar.dma_start(out=pqs_raw[i][:].rearrange("p (g t) -> p g t", t=T), in_=v.rearrange("(g p t) -> p g t", p=P, t=T))
+        def bank_tile():
+            return psum.tile([P, 512], F32, name="bank")
+
+        pqs_raw = keep.tile([P, 3, 2 * G * T], BF16, name="pqs_raw")
+        for i, v in enumerate((p, q, s)):
+            nc.scalar.dma_start(out=pqs_raw[:, i, 0:G * T].rearrange("p (g t) -> p g t", t=T), in_=v.rearrange("(g p t) -> p g t", p=P, t=T))
         w_scale = keep.tile([P, T], F32, name="w_scale")
         nc.scalar.dma_start(out=w_scale[:], in_=w2_scale.rearrange("o (p t) -> p (o t)", t=T))
         w_raw = keep.tile([P, 8 * O], U8, name="w_raw")
         w_view = w2_bytes.rearrange("(r p) k -> p r k", p=P)
+        g_view = g.rearrange("(g p t) k -> g p t k", p=P, t=T)
+        a_view = a.rearrange("(g p t) k -> g p t k", p=P, t=T)
+        x_view = x.rearrange("(g p t) k -> g p t k", p=P, t=T)
+        g_raw = [keep.tile([P, T, O], BF16, name="g_raw%d" % i) for i in range(G)]
+        a_raw = [keep.tile([P, T, H], BF16, name="a_raw%d" % i) for i in range(G)]
+        x_raw = [keep.tile([P, T, D], BF16, name="x_raw%d" % i) for i in range(G)]
 
         def load_w(i):
             nc.sync.dma_start(out=w_raw[:, i * 2048:(i + 1) * 2048].rearrange("p (r k) -> p r k", k=O), in_=w_view[:, 4 * i:4 * i + 4, :])
 
-        g_raw = [keep.tile([P, T, O], BF16, name="g_raw%d" % i) for i in range(G)]
-        a_raw = [keep.tile([P, T, H], BF16, name="a_raw%d" % i) for i in range(G)]
-        x_raw = [keep.tile([P, T, D], BF16, name="x_raw%d" % i) for i in range(G)]
-        g_view = g.rearrange("(g p t) k -> g p t k", p=P, t=T)
-        a_view = a.rearrange("(g p t) k -> g p t k", p=P, t=T)
-        x_view = x.rearrange("(g p t) k -> g p t k", p=P, t=T)
+        def load(tiles, view, i, c0=0, c1=None):
+            nc.sync.dma_start(out=tiles[i][:, :, c0:c1], in_=view[i][:, :, c0:c1])
+
         load_w(0)
         load_w(1)
-        nc.sync.dma_start(out=a_raw[0][:, :, 0:512], in_=a_view[0][:, :, 0:512])
-        nc.sync.dma_start(out=g_raw[0][:], in_=g_view[0])
-        nc.sync.dma_start(out=x_raw[0][:, :, 0:512], in_=x_view[0][:, :, 0:512])
-        nc.sync.dma_start(out=a_raw[1][:], in_=a_view[1])
-        nc.sync.dma_start(out=g_raw[1][:], in_=g_view[1])
-        nc.sync.dma_start(out=x_raw[1][:], in_=x_view[1])
-        nc.sync.dma_start(out=a_raw[0][:, :, 512:1024], in_=a_view[0][:, :, 512:1024])
-        nc.sync.dma_start(out=x_raw[0][:, :, 512:1024], in_=x_view[0][:, :, 512:1024])
+        load(a_raw, a_view, 0)
+        load(g_raw, g_view, 0)
+        load(x_raw, x_view, 0)
+        load(a_raw, a_view, 1)
+        load(g_raw, g_view, 1)
+        load(x_raw, x_view, 1)
+
         warm = keep.tile([P, 1], F32, name="warm")
         nc.vector.memset(warm[:], 0.0)
         nc.scalar.activation(out=warm[:], in_=warm[:], func=ACT.Tanh)
-
         ident = keep.tile([P, P], F32, name="ident")
         make_identity(nc, ident[:])
+        ident_bf = keep.tile([P, P], BF16, name="ident_bf")
+        nc.vector.tensor_copy(out=ident_bf[:], in_=ident[:])
 
         quarter = keep.tile([P, 2 * G * T], F32, name="quarter")
         nc.gpsimd.memset(quarter[:], 0.25)
         pqs = keep.tile([P, 3, G * T], F32, name="pqs")
-        for i, j in ((2, 0), (0, 1), (1, 2)):
-            nc.vector.tensor_copy(out=pqs[:, i, :], in_=pqs_raw[j][:])
+        nc.vector.tensor_copy(out=pqs[:], in_=pqs_raw[:, :, 0:G * T])
         weight = keep.tile([P, 2, G * T], F32, name="weight")
         nc.vector.tensor_tensor(out=weight[:], in0=pqs[:, 0:2, :], in1=pqs[:, 2:3, :].to_broadcast([P, 2, G * T]), op=ALU.mult)
         magnitude = keep.tile([P, 2, G * T], F32, name="magnitude")
@@ -76,18 +81,24 @@ def tile_diagonalfishernaturalgradient_kernel(tc, x, a, g, w2_bytes, w2_scale, p
         root4 = keep.tile([P, 2, G * T], F32, name="root4")
         nc.gpsimd.tensor_tensor(out=root4[:].rearrange("p a j -> p (a j)"), in0=magnitude[:].rearrange("p a j -> p (a j)"), in1=quarter[:], op=ALU.pow)
         root2 = keep.tile([P, 2, G * T], F32, name="root2")
-        nc.vector.tensor_tensor(out=root2[:], in0=root4[:], in1=root4[:], op=ALU.mult)
         f_inv = keep.tile([P, G * T], F32, name="f_inv")
-        nc.vector.reciprocal(out=f_inv[:], in_=root2[:, 1, :])
         neg_c = keep.tile([P, G * T], F32, name="neg_c")
-        nc.vector.scalar_tensor_tensor(out=neg_c[:], in0=f_inv[:], scalar=-1.0, in1=pqs[:, 1, :], op0=ALU.mult, op1=ALU.mult)
         r_hi = keep.tile([P, G * T], BF16, name="r_hi")
-        nc.vector.tensor_copy(out=r_hi[:], in_=root2[:, 0, :])
         r_lo = keep.tile([P, G * T], F32, name="r_lo")
-        nc.vector.tensor_tensor(out=r_lo[:], in0=root2[:, 0, :], in1=r_hi[:], op=ALU.subtract)
+
+        def finish_factors():
+            nc.vector.tensor_tensor(out=root2[:], in0=root4[:], in1=root4[:], op=ALU.mult)
+            nc.vector.reciprocal(out=f_inv[:], in_=root2[:, 1, :])
+            nc.vector.tensor_copy(out=r_hi[:], in_=root2[:, 0, :])
+            nc.vector.scalar_tensor_tensor(out=neg_c[:], in0=f_inv[:], scalar=-1.0, in1=pqs[:, 1, :], op0=ALU.mult, op1=ALU.mult)
+            nc.vector.tensor_tensor(out=r_lo[:], in0=root2[:, 0, :], in1=r_hi[:], op=ALU.subtract)
+
         diag = keep.tile([P, 2, G * T, P], BF16, name="diag")
-        for i, r in enumerate((r_hi, r_lo)):
-            nc.gpsimd.tensor_tensor(out=diag[:, i], in0=ident[:].unsqueeze(1).to_broadcast([P, G * T, P]), in1=r[:].unsqueeze(2).to_broadcast([P, G * T, P]), op=ALU.mult)
+
+        def make_diag(i):
+            js = slice(i * T, (i + 1) * T)
+            for k, r in enumerate((root2[:, 0, js], r_lo[:, js])):
+                nc.gpsimd.tensor_tensor(out=diag[:, k, js, :], in0=ident_bf[:].unsqueeze(1).to_broadcast([P, T, P]), in1=r.unsqueeze(2).to_broadcast([P, T, P]), op=ALU.mult)
 
         w_wide = keep.tile([P, 8 * O], BF16, name="w_wide")
         w_codes = keep.tile([P, H], U32, name="w_codes", align_bytes=64)
@@ -95,234 +106,376 @@ def tile_diagonalfishernaturalgradient_kernel(tc, x, a, g, w2_bytes, w2_scale, p
         scale_pair = w_scale[:].rearrange("p (u e) -> p u e", e=2).unsqueeze(1).to_broadcast([P, 256, 2, 2])
         w_il = {}
 
-        def cast_w(hh):
+        def cast_w(hh, copy):
             half = slice(hh * 2048, (hh + 1) * 2048)
-            nc.scalar.copy(out=w_wide[:, half], in_=w_raw[:, half].bitcast(FP8))
+            copy(out=w_wide[:, half], in_=w_raw[:, half].bitcast(FP8))
 
-        def turn_w(hh, b):
-            if b == 0:
-                w_il[hh] = stage.tile([P, HH, T], BF16, name="w_il", align_bytes=64)
-            bank = psa.tile([P, 512], F32, name="psa")
+        w_banks = {}
+
+        def turn_w(b):
+            bank = bank_tile()
+            w_banks[b] = bank
             for rr in range(2):
-                r = 4 * hh + 2 * b + rr
+                r = 2 * b + rr
                 words = w_wide[:, r * O:(r + 1) * O].bitcast(F32)
                 for u in range(2):
                     nc.tensor.transpose(bank[:, u * 256 + rr * P:u * 256 + (rr + 1) * P], words[:, u::2], ident[:])
+
+        def scale_w(b):
+            if b % 2 == 0:
+                w_il[b // 2] = stage.tile([P, 512, T], BF16, name="w_il", tag="head_il", bufs=3, align_bytes=64)
             nc.vector.tensor_tensor(
-                out=w_il[hh][:, b * 256:(b + 1) * 256, :].rearrange("p h (u e) -> p h u e", e=2),
-                in0=bank[:].bitcast(BF16).rearrange("p (u h e) -> p h u e", u=2, e=2),
+                out=w_il[b // 2][:, (b % 2) * 256:(b % 2 + 1) * 256, :].rearrange("p h (u e) -> p h u e", e=2),
+                in0=w_banks[b][:].bitcast(BF16).rearrange("p (u h e) -> p h u e", u=2, e=2),
                 in1=scale_pair, op=ALU.mult)
 
         def quant_w(hh):
-            cols = slice(hh * HH, (hh + 1) * HH)
+            cols = slice(hh * 512, (hh + 1) * 512)
             nc.vector.quantize_mx(out=w_codes[:, cols].bitcast(FP8X4), scales=w_scales[:, cols], in_=w_il[hh][:].rearrange("p h t -> p (h t)"))
 
         g_codes = keep.tile([P, G, 512], U32, name="g_codes", align_bytes=64)
         g_scales = keep.tile([P, G, 512], U8, name="g_scales", align_bytes=64)
-
         g_ils = {}
 
-        def turn_g(i):
-            g_il = stage.tile([P, T * P, T], BF16, name="g_il", align_bytes=64)
-            g_ils[i] = g_il
-            for b in range(2):
-                bank = psa.tile([P, 512], F32, name="psa")
-                for tt in range(2):
-                    words = g_raw[i][:, 2 * b + tt, :].bitcast(F32)
-                    for u in range(2):
-                        nc.tensor.transpose(bank[:, (2 * tt + u) * P:(2 * tt + u + 1) * P], words[:, u::2], ident[:])
-                nc.scalar.copy(
-                    out=g_il[:, b * 256:(b + 1) * 256, :].rearrange("p n t -> p (n t)").bitcast(F32).rearrange("p (t m u) -> p t m u", t=2, u=2),
-                    in_=bank[:].rearrange("p (t u m) -> p t m u", t=2, u=2))
+        g_banks = {}
+
+        def turn_g(i, b):
+            bank = bank_tile()
+            g_banks[i, b] = bank
+            for tt in range(2):
+                words = g_raw[i][:, 2 * b + tt, :].bitcast(F32)
+                for u in range(2):
+                    nc.tensor.transpose(bank[:, (2 * tt + u) * P:(2 * tt + u + 1) * P], words[:, u::2], ident[:])
+
+        def weave_g(i, b, copy):
+            if b == 0:
+                g_ils[i] = stage.tile([P, T * P, T], BF16, name="g_il", tag="head_il", bufs=3, align_bytes=64)
+            copy(
+                out=g_ils[i][:, b * 256:(b + 1) * 256, :].rearrange("p n t -> p (n t)").bitcast(F32).rearrange("p (t m u) -> p t m u", t=2, u=2),
+                in_=g_banks[i, b][:].rearrange("p (t u m) -> p t m u", t=2, u=2))
 
         def quant_g(i):
             nc.vector.quantize_mx(out=g_codes[:, i, :].bitcast(FP8X4), scales=g_scales[:, i, :], in_=g_ils[i][:].rearrange("p n t -> p (n t)"))
 
-        xp_codes = keep.tile([P, G, D], U32, name="xp_codes", align_bytes=64)
-        xp_scales = keep.tile([P, G, D], U8, name="xp_scales", align_bytes=64)
-        x2_codes = keep.tile([P, G, D], U32, name="x2_codes", align_bytes=64)
-        x2_scales = keep.tile([P, G, D], U8, name="x2_scales", align_bytes=64)
-
+        xp_codes = [keep.tile([P, G, w], U32, name="xp_codes%d" % c0, align_bytes=64) for c0, w in X_CHUNKS]
+        xp_scales = [keep.tile([P, G, w], U8, name="xp_scales%d" % c0, align_bytes=64) for c0, w in X_CHUNKS]
+        x2_codes = [keep.tile([P, G, w], U32, name="x2_codes%d" % c0, align_bytes=64) for c0, w in X_CHUNKS]
+        x2_scales = [keep.tile([P, G, w], U8, name="x2_scales%d" % c0, align_bytes=64) for c0, w in X_CHUNKS]
+        xp_planar = [keep.tile([P, T, D], BF16, name="xp_planar%d" % i) for i in range(G)]
         xp_ils = {}
         x2_ils = {}
+        x2_banks = {}
 
-        def make_xp(i, half):
-            cols = slice(half * 512, half * 512 + 512)
-            planar = stage.tile([P, T, 512], BF16, name="xp_planar")
+        def scale_x(i):
             for t in range(T):
-                nc.vector.tensor_scalar(out=planar[:, t, :], in0=x_raw[i][:, t, cols], scalar1=pqs[:, 0, i * T + t:i * T + t + 1], scalar2=None, op0=ALU.mult)
-            il = stage.tile([P, 512, T], BF16, name="xp_il", align_bytes=64)
-            xp_ils[i, half] = il
-            nc.vector.tensor_copy(out=il[:], in_=planar[:].rearrange("p t d -> p d t"))
+                nc.vector.tensor_scalar(out=xp_planar[i][:, t, :], in0=x_raw[i][:, t, :], scalar1=pqs[:, 0, i * T + t:i * T + t + 1], scalar2=None, op0=ALU.mult)
 
-        def quant_xp(i, half):
-            cols = slice(half * 512, half * 512 + 512)
-            il = xp_ils[i, half]
-            nc.vector.quantize_mx(out=xp_codes[:, i, cols].bitcast(FP8X4), scales=xp_scales[:, i, cols], in_=il[:].rearrange("p d t -> p (d t)"))
+        def weave_xp(j, i):
+            c0, w = X_CHUNKS[j]
+            if i == 0:
+                xp_ils[j] = stage.tile([P, G, w, T], BF16, name="xp_il", tag="il", bufs=5, align_bytes=64)
+            nc.vector.tensor_copy(out=xp_ils[j][:, i].rearrange("p (c i) t -> p c t i", i=4), in_=xp_planar[i][:, :, c0:c0 + w].rearrange("p t (c i) -> p c t i", i=4))
 
-        def make_x2(i, half):
-            il = stage.tile([P, 512, T], BF16, name="x2_il", align_bytes=64)
-            x2_ils[i, half] = il
-            for b in range(4):
-                bank = psa.tile([P, 512], F32, name="psa")
+        def quantize(codes, scales, j, il):
+            nc.vector.quantize_mx(
+                out=codes[j][:].rearrange("p g c -> p (g c)").bitcast(FP8X4),
+                scales=scales[j][:].rearrange("p g c -> p (g c)"),
+                in_=il[:].rearrange("p g c t -> p (g c t)"))
+
+        def quant_xp(j):
+            quantize(xp_codes, xp_scales, j, xp_ils[j])
+
+        def mul_x2(j, i):
+            c0, w = X_CHUNKS[j]
+            for b in range(w // P):
+                bank = bank_tile()
+                x2_banks[j, i, b] = bank
+                cols = slice(c0 + b * P, c0 + (b + 1) * P)
                 for t in range(T):
-                    cols = slice(half * 512 + b * DC, half * 512 + (b + 1) * DC)
                     for k in range(2):
-                        nc.tensor.matmul(bank[:, t * DC:(t + 1) * DC], lhsT=diag[:, k, i * T + t, :], rhs=x_raw[i][:, t, cols], start=(k == 0), stop=(k == 1))
-                nc.scalar.activation(out=il[:, b * DC:(b + 1) * DC, :], in_=bank[:].rearrange("p (t d) -> p d t", t=T), func=ACT.Square)
+                        nc.tensor.matmul(bank[:, t * P:(t + 1) * P], lhsT=diag[:, k, i * T + t, :], rhs=x_raw[i][:, t, cols], start=(k == 0), stop=(k == 1))
 
-        def quant_x2(i, half):
-            cols = slice(half * 512, half * 512 + 512)
-            il = x2_ils[i, half]
-            nc.vector.quantize_mx(out=x2_codes[:, i, cols].bitcast(FP8X4), scales=x2_scales[:, i, cols], in_=il[:].rearrange("p d t -> p (d t)"))
+        def square_x2(j, i):
+            c0, w = X_CHUNKS[j]
+            if i == 0:
+                x2_ils[j] = stage.tile([P, G, w, T], BF16, name="x2_il", tag="il", bufs=5, align_bytes=64)
+            for b in range(w // P):
+                nc.scalar.activation(out=x2_ils[j][:, i, b * P:(b + 1) * P, :], in_=x2_banks[j, i, b][:].rearrange("p (t d) -> p d t", t=T), func=ACT.Square)
 
-        dq_codes = keep.tile([P, G, H], U32, name="dq_codes", align_bytes=64)
-        dq_scales = keep.tile([P, G, H], U8, name="dq_scales", align_bytes=64)
-        d2_codes = keep.tile([P, G, H], U32, name="d2_codes", align_bytes=64)
-        d2_scales = keep.tile([P, G, H], U8, name="d2_scales", align_bytes=64)
-        th = {}
+        def quant_x2(j):
+            quantize(x2_codes, x2_scales, j, x2_ils[j])
 
-        def make_tanh(i, hh):
-            th[i, hh] = keep.tile([P, T, HH], F32, name="th%d%d" % (i, hh))
-            nc.scalar.activation(out=th[i, hh][:], in_=a_raw[i][:, :, hh * HH:(hh + 1) * HH], func=ACT.Tanh)
+        dq_codes = [keep.tile([P, G, w], U32, name="dq_codes%d" % c0, align_bytes=64) for c0, w in D_CHUNKS]
+        dq_scales = [keep.tile([P, G, w], U8, name="dq_scales%d" % c0, align_bytes=64) for c0, w in D_CHUNKS]
+        d2_codes = [keep.tile([P, G, w], U32, name="d2_codes%d" % c0, align_bytes=64) for c0, w in D_CHUNKS]
+        d2_scales = [keep.tile([P, G, w], U8, name="d2_scales%d" % c0, align_bytes=64) for c0, w in D_CHUNKS]
+        th = [keep.tile([P, T, H], F32, name="th%d" % i) for i in range(G)]
+        back_banks = {}
+        dq_ils = {}
+        d2_ils = {}
 
-        def make_sech(i, hh):
+        def tanh(i, c0=0, c1=H):
+            nc.scalar.activation(out=th[i][:, :, c0:c1], in_=a_raw[i][:, :, c0:c1], func=ACT.Tanh)
+
+        def sech(hh, i):
             for t in range(T):
                 j = i * T + t
-                nc.scalar.activation(out=th[i, hh][:, t, :], in_=th[i, hh][:, t, :], func=ACT.Square, scale=root4[:, 1, j:j + 1])
+                sq = th[i][:, t, hh * 512:(hh + 1) * 512]
+                nc.scalar.activation(out=sq, in_=sq, func=ACT.Square, scale=root4[:, 1, j:j + 1])
 
-        def make_e(i, hh, t):
-            j = i * T + t
-            bank = psa.tile([P, 512], F32, name="psa")
-            nc.tensor.matmul_mx(
-                out=bank[:], lhsT=g_codes[:, i, t * P:(t + 1) * P].bitcast(FP8X4), lhsT_scale=g_scales[:, i, t * P:(t + 1) * P],
-                rhs=w_codes[:, hh * HH:(hh + 1) * HH].bitcast(FP8X4), rhs_scale=w_scales[:, hh * HH:(hh + 1) * HH], start=True, stop=True)
-            nc.vector.scalar_tensor_tensor(out=th[i, hh][:, t, :], in0=th[i, hh][:, t, :], scalar=root2[:, 1, j:j + 1], in1=bank[:], op0=ALU.subtract, op1=ALU.mult)
+        def mul_back(hh, i):
+            cols = slice(hh * 512, (hh + 1) * 512)
+            for t in range(T):
+                bank = bank_tile()
+                back_banks[hh, i, t] = bank
+                rows = slice(t * P, (t + 1) * P)
+                nc.tensor.matmul_mx(
+                    out=bank[:], lhsT=g_codes[:, i, rows].bitcast(FP8X4), lhsT_scale=g_scales[:, i, rows],
+                    rhs=w_codes[:, cols].bitcast(FP8X4), rhs_scale=w_scales[:, cols], start=True, stop=True)
 
-        d_ils = {}
+        def make_e(hh, i):
+            for t in range(T):
+                j = i * T + t
+                e = th[i][:, t, hh * 512:(hh + 1) * 512]
+                nc.vector.scalar_tensor_tensor(out=e, in0=e, scalar=root2[:, 1, j:j + 1], in1=back_banks[hh, i, t][:], op0=ALU.subtract, op1=ALU.mult)
 
-        def make_d(i, c0, w):
-            hh, off = divmod(c0, HH)
-            e = th[i, hh][:, :, off:off + w].rearrange("p t h -> p h t")
-            d2_il = stage.tile([P, w, T], BF16, name="d2_il", align_bytes=64)
-            dq_il = stage.tile([P, w, T], BF16, name="dq_il", align_bytes=64)
-            d_ils[i, c0] = (dq_il, d2_il)
-            nc.scalar.activation(out=d2_il[:], in_=e, func=ACT.Square)
-            nc.vector.tensor_tensor(out=dq_il[:], in0=e, in1=neg_c[:, i * T:(i + 1) * T].unsqueeze(1).to_broadcast([P, w, T]), op=ALU.mult)
+        def square_d(c, i):
+            c0, w = D_CHUNKS[c]
+            if i == 0:
+                d2_ils[c] = stage.tile([P, G, w, T], BF16, name="d2_il", tag="il", bufs=5, align_bytes=64)
+            e = th[i][:, :, c0:c0 + w].rearrange("p t (c i) -> p c t i", i=4)
+            nc.scalar.activation(out=d2_ils[c][:, i].rearrange("p (c i) t -> p c t i", i=4), in_=e, func=ACT.Square)
 
-        def quant_d(i, c0, w):
-            cols = slice(c0, c0 + w)
-            dq_il, d2_il = d_ils[i, c0]
-            nc.vector.quantize_mx(out=d2_codes[:, i, cols].bitcast(FP8X4), scales=d2_scales[:, i, cols], in_=d2_il[:].rearrange("p h t -> p (h t)"))
-            nc.vector.quantize_mx(out=dq_codes[:, i, cols].bitcast(FP8X4), scales=dq_scales[:, i, cols], in_=dq_il[:].rearrange("p h t -> p (h t)"))
+        def weave_dq(c, i):
+            c0, w = D_CHUNKS[c]
+            if i == 0:
+                dq_ils[c] = stage.tile([P, G, w, T], BF16, name="dq_il", tag="il", bufs=5, align_bytes=64)
+            e = th[i][:, :, c0:c0 + w].rearrange("p t (c i) -> p c t i", i=4)
+            factor = neg_c[:, i * T:(i + 1) * T].unsqueeze(1).unsqueeze(3).to_broadcast([P, w // 4, T, 4])
+            nc.vector.tensor_tensor(out=dq_ils[c][:, i].rearrange("p (c i) t -> p c t i", i=4), in0=e, in1=factor, op=ALU.mult)
+
+        def quant_d2(c):
+            quantize(d2_codes, d2_scales, c, d2_ils[c])
+
+        def quant_dq(c):
+            quantize(dq_codes, dq_scales, c, dq_ils[c])
 
         live = {}
 
-        def product(m, c0, w, lc, ls, rc, rs):
-            cols = slice(c0, c0 + w)
-            bank = psa.tile([P, 512], F32, name="psa")
+        def product(j, c, m, lc, ls, rc, rs):
+            w = D_CHUNKS[c][1]
+            bank = bank_tile()
             for b in range(512 // w):
                 rows = slice((m + b) * P, (m + b + 1) * P)
                 for i in range(G):
-                    nc.tensor.matmul_mx(out=bank[:, b * w:(b + 1) * w], lhsT=lc[:, i, rows].bitcast(FP8X4), lhsT_scale=ls[:, i, rows], rhs=rc[:, i, cols].bitcast(FP8X4), rhs_scale=rs[:, i, cols], start=(i == 0), stop=(i == G - 1))
+                    nc.tensor.matmul_mx(
+                        out=bank[:, b * w:(b + 1) * w], lhsT=lc[j][:, i, rows].bitcast(FP8X4), lhsT_scale=ls[j][:, i, rows],
+                        rhs=rc[c][:, i, :].bitcast(FP8X4), rhs_scale=rs[c][:, i, :], start=(i == 0), stop=(i == G - 1))
             return bank
 
-        def open_tile(m, c0, w):
-            fish = product(m, c0, w, x2_codes, x2_scales, d2_codes, d2_scales)
-            inv_root = stage.tile([P, 512], F32, name="inv_root", bufs=3)
-            nc.scalar.activation(out=inv_root[:], in_=fish[:], func=ACT.Abs_reciprocal_sqrt, scale=1.0 / 32.0, bias=6.4)
-            live[m, c0] = inv_root
+        def mul_fish(*k):
+            live[k, "fish"] = product(*k, x2_codes, x2_scales, d2_codes, d2_scales)
 
-        def close_tile(m, c0, w, on_vector):
-            grad = product(m, c0, w, xp_codes, xp_scales, dq_codes, dq_scales)
-            inv_root = live[m, c0]
+        def mul_grad(*k):
+            live[k, "grad"] = product(*k, xp_codes, xp_scales, dq_codes, dq_scales)
+
+        def root(*k):
+            live[k, "root"] = stage.tile([P, 512], F32, name="inv_root", bufs=4)
+            nc.scalar.activation(out=live[k, "root"][:], in_=live[k, "fish"][:], func=ACT.Abs_reciprocal_sqrt, scale=1.0 / 32.0, bias=6.4)
+
+        def divide(*k):
+            live[k, "inv"] = stage.tile([P, 512], F32, name="inv")
+            nc.scalar.activation(out=live[k, "inv"][:], in_=live[k, "root"][:], func=ACT.Square)
+
+        def g_divide(*k):
+            live[k, "inv"] = stage.tile([P, 512], F32, name="ginv")
+            nc.gpsimd.tensor_tensor(out=live[k, "inv"][:], in0=live[k, "root"][:], in1=live[k, "root"][:], op=ALU.mult)
+
+        def finish(*k):
             res = stage.tile([P, 512], F32, name="res", bufs=4)
-            if on_vector:
-                part = stage.tile([P, 512], F32, name="part")
-                nc.vector.tensor_tensor(out=part[:], in0=grad[:], in1=inv_root[:], op=ALU.mult)
-                nc.vector.tensor_tensor(out=res[:], in0=part[:], in1=inv_root[:], op=ALU.mult)
-            else:
-                inv = stage.tile([P, 512], F32, name="inv")
-                nc.scalar.activation(out=inv[:], in_=inv_root[:], func=ACT.Square)
-                nc.vector.tensor_tensor(out=res[:], in0=grad[:], in1=inv[:], op=ALU.mult)
-            blocks = 512 // w
+            nc.vector.tensor_tensor(out=res[:], in0=live[k, "grad"][:], in1=live[k, "inv"][:], op=ALU.mult)
+            store_tile(*k, res)
+
+        def half_finish(*k):
+            live[k, "part"] = stage.tile([P, 512], F32, name="part")
+            nc.vector.tensor_tensor(out=live[k, "part"][:], in0=live[k, "grad"][:], in1=live[k, "root"][:], op=ALU.mult)
+
+        def rest_finish(*k):
+            res = stage.tile([P, 512], F32, name="res", bufs=4)
+            nc.vector.tensor_tensor(out=res[:], in0=live[k, "part"][:], in1=live[k, "root"][:], op=ALU.mult)
+            store_tile(*k, res)
+
+        def store_tile(j, c, m, res):
+            x0 = X_CHUNKS[j][0] + m * P
+            c0, w = D_CHUNKS[c]
+            n = 512 // w
             nc.sync.dma_start(
-                out=out[m * P:(m + blocks) * P, c0:c0 + w].rearrange("(b p) h -> p b h", p=P),
-                in_=res[:].rearrange("p (b h) -> p b h", b=blocks))
+                out=out[x0:x0 + n * P, c0:c0 + w].rearrange("(b p) h -> p b h", p=P),
+                in_=res[:].rearrange("p (b h) -> p b h", b=n))
 
         ctx.enter_context(tc.manual_schedule())
-        cast_w(0)
-        turn_w(0, 0)
-        cast_w(1)
-        turn_w(0, 1)
-        make_tanh(0, 0)
-        turn_w(1, 0)
-        turn_w(1, 1)
-        turn_g(0)
+        cast_w(0, nc.scalar.copy)
+        cast_w(1, nc.vector.tensor_copy)
+        finish_factors()
+        make_diag(0)
+        tanh(0, 0, 512)
+        sech(0, 0)
+        turn_w(0)
+        scale_w(0)
+        turn_w(1)
+        scale_w(1)
+        turn_w(2)
+        turn_w(3)
+        scale_w(2)
+        scale_w(3)
+        tanh(0, 512, 1024)
+        scale_x(0)
         quant_w(0)
-        make_sech(0, 0)
-        make_xp(0, 0)
-        make_tanh(1, 0)
-        quant_g(0)
-        make_x2(0, 0)
-        for t in range(T):
-            make_e(0, 0, t)
+        turn_g(0, 0)
+        weave_g(0, 0, nc.scalar.copy)
+        turn_g(0, 1)
+        weave_g(0, 1, nc.vector.tensor_copy)
+        mul_x2(0, 0)
+        square_x2(0, 0)
+        weave_xp(0, 0)
         quant_w(1)
-        quant_xp(0, 0)
-        turn_g(1)
-        make_sech(1, 0)
-        make_d(0, 0, 512)
-        quant_x2(0, 0)
+        weave_xp(1, 0)
+        turn_g(1, 0)
+        turn_g(1, 1)
+        weave_g(1, 0, nc.scalar.copy)
+        weave_g(1, 1, nc.vector.tensor_copy)
+        scale_x(1)
+        tanh(1, 0, 512)
+        sech(0, 1)
+        quant_g(0)
+        weave_xp(0, 1)
         quant_g(1)
-        for t in range(T):
-            make_e(1, 0, t)
-        make_x2(1, 0)
-        quant_d(0, 0, 512)
-        make_d(1, 0, 512)
-        make_xp(1, 0)
-        make_tanh(0, 1)
-        make_tanh(1, 1)
-        quant_x2(1, 0)
-        quant_d(1, 0, 512)
-        quant_xp(1, 0)
-        make_xp(0, 1)
-        make_xp(1, 1)
-        quant_xp(0, 1)
-        quant_xp(1, 1)
-
-        def side(k):
-            if k == 0:
-                make_x2(0, 1)
-            if k == 1:
-                make_x2(1, 1)
-                quant_x2(0, 1)
-            if k == 2:
-                make_sech(0, 1)
-                for t in range(T):
-                    make_e(0, 1, t)
-            if k == 3:
-                make_sech(1, 1)
-                quant_x2(1, 1)
-                for t in range(T):
-                    make_e(1, 1, t)
-            if k == 4:
-                make_d(0, 512, 256)
-                make_d(1, 512, 256)
-            if k == 5:
-                quant_d(0, 512, 256)
-                quant_d(1, 512, 256)
-            if k == 6:
-                make_d(0, 768, 256)
-            if k == 7:
-                make_d(1, 768, 256)
-            if k == 8:
-                quant_d(0, 768, 256)
-                quant_d(1, 768, 256)
-
-        order = [(m, 0, 512) for m in range(8)] + [(m, c0, 256) for c0 in (512, 768) for m in range(0, 8, 2)]
-        for k in range(17):
-            if k < 16:
-                open_tile(*order[k])
-            if k > 0:
-                close_tile(*order[k - 1], on_vector=(k % 2 == 0))
-            side(k)
+        weave_xp(1, 1)
+        make_diag(1)
+        mul_x2(0, 1)
+        square_x2(0, 1)
+        mul_back(0, 0)
+        make_e(0, 0)
+        mul_x2(1, 0)
+        square_x2(1, 0)
+        mul_x2(1, 1)
+        square_x2(1, 1)
+        quant_xp(0)
+        quant_xp(1)
+        tanh(1, 512, 1024)
+        quant_x2(0)
+        mul_back(0, 1)
+        mul_back(1, 0)
+        make_e(0, 1)
+        square_d(0, 0)
+        square_d(0, 1)
+        quant_x2(1)
+        mul_back(1, 1)
+        weave_dq(0, 0)
+        weave_dq(0, 1)
+        sech(1, 0)
+        make_e(1, 0)
+        quant_d2(0)
+        sech(1, 1)
+        make_e(1, 1)
+        mul_x2(2, 0)
+        square_x2(2, 0)
+        weave_dq(1, 0)
+        weave_dq(1, 1)
+        square_d(1, 0)
+        square_d(1, 1)
+        mul_x2(2, 1)
+        mul_fish(0, 0, 3)
+        root(0, 0, 3)
+        divide(0, 0, 3)
+        mul_fish(0, 0, 1)
+        root(0, 0, 1)
+        quant_dq(0)
+        mul_grad(0, 0, 0)
+        mul_fish(0, 0, 0)
+        quant_d2(1)
+        mul_grad(0, 0, 3)
+        square_x2(2, 1)
+        weave_dq(2, 0)
+        weave_dq(2, 1)
+        square_d(2, 0)
+        quant_dq(1)
+        mul_fish(0, 0, 2)
+        finish(0, 0, 3)
+        mul_fish(0, 1, 2)
+        mul_grad(0, 0, 2)
+        mul_fish(1, 0, 1)
+        mul_fish(1, 0, 0)
+        root(0, 0, 2)
+        half_finish(0, 0, 2)
+        root(0, 0, 0)
+        half_finish(0, 0, 0)
+        rest_finish(0, 0, 2)
+        square_d(2, 1)
+        quant_d2(2)
+        root(0, 1, 2)
+        mul_grad(0, 1, 2)
+        divide(0, 0, 1)
+        mul_grad(1, 0, 0)
+        mul_grad(1, 1, 0)
+        half_finish(0, 1, 2)
+        quant_dq(2)
+        root(1, 0, 1)
+        mul_fish(0, 1, 0)
+        rest_finish(0, 1, 2)
+        mul_fish(1, 1, 0)
+        rest_finish(0, 0, 0)
+        mul_grad(0, 0, 1)
+        finish(0, 0, 1)
+        root(1, 0, 0)
+        divide(1, 0, 0)
+        finish(1, 0, 0)
+        root(0, 1, 0)
+        divide(0, 1, 0)
+        mul_grad(0, 1, 0)
+        quant_x2(2)
+        weave_xp(2, 0)
+        mul_fish(0, 2, 0)
+        mul_grad(1, 0, 1)
+        root(1, 1, 0)
+        mul_fish(1, 2, 0)
+        half_finish(1, 1, 0)
+        finish(0, 1, 0)
+        mul_fish(0, 2, 2)
+        mul_grad(0, 2, 2)
+        divide(1, 0, 1)
+        finish(1, 0, 1)
+        root(1, 2, 0)
+        root(0, 2, 0)
+        divide(1, 2, 0)
+        rest_finish(1, 1, 0)
+        root(0, 2, 2)
+        weave_xp(2, 1)
+        mul_grad(1, 2, 0)
+        finish(1, 2, 0)
+        half_finish(0, 2, 2)
+        divide(0, 2, 0)
+        quant_xp(2)
+        mul_fish(2, 0, 0)
+        root(2, 0, 0)
+        mul_fish(2, 0, 1)
+        root(2, 0, 1)
+        mul_fish(2, 2, 0)
+        mul_grad(0, 2, 0)
+        mul_fish(2, 1, 0)
+        finish(0, 2, 0)
+        mul_grad(2, 0, 0)
+        mul_grad(2, 0, 1)
+        rest_finish(0, 2, 2)
+        divide(2, 0, 0)
+        root(2, 2, 0)
+        finish(2, 0, 0)
+        divide(2, 2, 0)
+        mul_grad(2, 1, 0)
+        half_finish(2, 0, 1)
+        rest_finish(2, 0, 1)
+        root(2, 1, 0)
+        divide(2, 1, 0)
+        finish(2, 1, 0)
+        mul_grad(2, 2, 0)
+        finish(2, 2, 0)

@@ -49,17 +49,19 @@ def tile_diagonalfishernaturalgradient_kernel(tc, x, a, g, w2_bytes, w2_scale, p
         def load_w(i):
             nc.sync.dma_start(out=w_raw[:, i * 2048:(i + 1) * 2048].rearrange("p (r k) -> p r k", k=O), in_=w_view[:, 4 * i:4 * i + 4, :])
 
-        def load(tiles, view, i, c0=0, c1=None):
-            nc.sync.dma_start(out=tiles[i][:, :, c0:c1], in_=view[i][:, :, c0:c1])
+        def load(tiles, view, i, t0, t1):
+            nc.sync.dma_start(out=tiles[i][:, t0:t1], in_=view[i][:, t0:t1])
 
         load_w(0)
         load_w(1)
-        load(a_raw, a_view, 0)
-        load(g_raw, g_view, 0)
-        load(x_raw, x_view, 0)
-        load(a_raw, a_view, 1)
-        load(g_raw, g_view, 1)
-        load(x_raw, x_view, 1)
+        load(a_raw, a_view, 0, 0, 2)
+        load(x_raw, x_view, 0, 0, 2)
+        load(a_raw, a_view, 0, 2, 4)
+        load(g_raw, g_view, 0, 0, 4)
+        load(x_raw, x_view, 0, 2, 4)
+        load(a_raw, a_view, 1, 0, 4)
+        load(g_raw, g_view, 1, 0, 4)
+        load(x_raw, x_view, 1, 0, 4)
 
         warm = keep.tile([P, 1], F32, name="warm")
         nc.vector.memset(warm[:], 0.0)
@@ -142,14 +144,14 @@ def tile_diagonalfishernaturalgradient_kernel(tc, x, a, g, w2_bytes, w2_scale, p
         def turn_g(i, b):
             bank = bank_tile()
             g_banks[i, b] = bank
+            if b == 0:
+                g_ils[i] = stage.tile([P, T * P, T], BF16, name="g_il", tag="head_il", bufs=3, align_bytes=64)
             for tt in range(2):
                 words = g_raw[i][:, 2 * b + tt, :].bitcast(F32)
                 for u in range(2):
                     nc.tensor.transpose(bank[:, (2 * tt + u) * P:(2 * tt + u + 1) * P], words[:, u::2], ident[:])
 
         def weave_g(i, b, copy):
-            if b == 0:
-                g_ils[i] = stage.tile([P, T * P, T], BF16, name="g_il", tag="head_il", bufs=3, align_bytes=64)
             copy(
                 out=g_ils[i][:, b * 256:(b + 1) * 256, :].rearrange("p n t -> p (n t)").bitcast(F32).rearrange("p (t m u) -> p t m u", t=2, u=2),
                 in_=g_banks[i, b][:].rearrange("p (t u m) -> p t m u", t=2, u=2))
@@ -166,15 +168,23 @@ def tile_diagonalfishernaturalgradient_kernel(tc, x, a, g, w2_bytes, w2_scale, p
         x2_ils = {}
         x2_banks = {}
 
-        def scale_x(i):
-            for t in range(T):
-                nc.vector.tensor_scalar(out=xp_planar[i][:, t, :], in0=x_raw[i][:, t, :], scalar1=pqs[:, 0, i * T + t:i * T + t + 1], scalar2=None, op0=ALU.mult)
+        def scale_x(i, t, engine):
+            engine.tensor_scalar(out=xp_planar[i][:, t, :], in0=x_raw[i][:, t, :], scalar1=pqs[:, 0, i * T + t:i * T + t + 1], scalar2=0.0, op0=ALU.mult, op1=ALU.add)
+
+        def open_xp(j):
+            xp_ils[j] = stage.tile([P, G, X_CHUNKS[j][1], T], BF16, name="xp_il", tag="il", bufs=5, align_bytes=64)
 
         def weave_xp(j, i):
             c0, w = X_CHUNKS[j]
-            if i == 0:
-                xp_ils[j] = stage.tile([P, G, w, T], BF16, name="xp_il", tag="il", bufs=5, align_bytes=64)
             nc.vector.tensor_copy(out=xp_ils[j][:, i].rearrange("p (c i) t -> p c t i", i=4), in_=xp_planar[i][:, :, c0:c0 + w].rearrange("p t (c i) -> p c t i", i=4))
+
+        def s_weave_xp(j, i):
+            c0, w = X_CHUNKS[j]
+            nc.scalar.copy(out=xp_ils[j][:, i].rearrange("p (c i) t -> p c t i", i=4), in_=xp_planar[i][:, :, c0:c0 + w].rearrange("p t (c i) -> p c t i", i=4))
+
+        def g_weave_xp(j, i):
+            c0, w = X_CHUNKS[j]
+            nc.gpsimd.tensor_scalar(out=xp_ils[j][:, i], in0=xp_planar[i][:, :, c0:c0 + w].rearrange("p t c -> p c t"), scalar1=1.0, scalar2=0.0, op0=ALU.mult, op1=ALU.add)
 
         def quantize(codes, scales, j, il):
             nc.vector.quantize_mx(
@@ -214,11 +224,11 @@ def tile_diagonalfishernaturalgradient_kernel(tc, x, a, g, w2_bytes, w2_scale, p
         dq_ils = {}
         d2_ils = {}
 
-        def tanh(i, c0=0, c1=H):
-            nc.scalar.activation(out=th[i][:, :, c0:c1], in_=a_raw[i][:, :, c0:c1], func=ACT.Tanh)
+        def tanh(i, t0):
+            nc.scalar.activation(out=th[i][:, t0:t0 + 2], in_=a_raw[i][:, t0:t0 + 2], func=ACT.Tanh)
 
-        def sech(hh, i):
-            for t in range(T):
+        def sech(hh, i, t0):
+            for t in range(t0, t0 + 2):
                 j = i * T + t
                 sq = th[i][:, t, hh * 512:(hh + 1) * 512]
                 nc.scalar.activation(out=sq, in_=sq, func=ACT.Square, scale=root4[:, 1, j:j + 1])
@@ -246,10 +256,17 @@ def tile_diagonalfishernaturalgradient_kernel(tc, x, a, g, w2_bytes, w2_scale, p
             e = th[i][:, :, c0:c0 + w].rearrange("p t (c i) -> p c t i", i=4)
             nc.scalar.activation(out=d2_ils[c][:, i].rearrange("p (c i) t -> p c t i", i=4), in_=e, func=ACT.Square)
 
+        def open_dq(c):
+            dq_ils[c] = stage.tile([P, G, D_CHUNKS[c][1], T], BF16, name="dq_il", tag="il", bufs=5, align_bytes=64)
+
+        def g_weave_dq(c, i):
+            c0, w = D_CHUNKS[c]
+            e = th[i][:, :, c0:c0 + w].rearrange("p t c -> p c t")
+            factor = neg_c[:, i * T:(i + 1) * T].unsqueeze(1).to_broadcast([P, w, T])
+            nc.gpsimd.tensor_tensor(out=dq_ils[c][:, i], in0=e, in1=factor, op=ALU.mult)
+
         def weave_dq(c, i):
             c0, w = D_CHUNKS[c]
-            if i == 0:
-                dq_ils[c] = stage.tile([P, G, w, T], BF16, name="dq_il", tag="il", bufs=5, align_bytes=64)
             e = th[i][:, :, c0:c0 + w].rearrange("p t (c i) -> p c t i", i=4)
             factor = neg_c[:, i * T:(i + 1) * T].unsqueeze(1).unsqueeze(3).to_broadcast([P, w // 4, T, 4])
             nc.vector.tensor_tensor(out=dq_ils[c][:, i].rearrange("p (c i) t -> p c t i", i=4), in0=e, in1=factor, op=ALU.mult)
@@ -288,12 +305,22 @@ def tile_diagonalfishernaturalgradient_kernel(tc, x, a, g, w2_bytes, w2_scale, p
             nc.scalar.activation(out=live[k, "inv"][:], in_=live[k, "root"][:], func=ACT.Square)
 
         def g_divide(*k):
-            live[k, "inv"] = stage.tile([P, 512], F32, name="ginv")
-            nc.gpsimd.tensor_tensor(out=live[k, "inv"][:], in0=live[k, "root"][:], in1=live[k, "root"][:], op=ALU.mult)
+            live[k, "ginv"] = stage.tile([P, 512], F32, name="ginv")
+            nc.gpsimd.tensor_tensor(out=live[k, "ginv"][:], in0=live[k, "root"][:], in1=live[k, "root"][:], op=ALU.mult)
 
         def finish(*k):
             res = stage.tile([P, 512], F32, name="res", bufs=4)
             nc.vector.tensor_tensor(out=res[:], in0=live[k, "grad"][:], in1=live[k, "inv"][:], op=ALU.mult)
+            store_tile(*k, res)
+
+        def g_rest_finish(*k):
+            res = stage.tile([P, 512], F32, name="res", bufs=4)
+            nc.gpsimd.tensor_tensor(out=res[:], in0=live[k, "part"][:], in1=live[k, "root"][:], op=ALU.mult)
+            store_tile(*k, res)
+
+        def g_finish(*k):
+            res = stage.tile([P, 512], F32, name="res", bufs=4)
+            nc.vector.tensor_tensor(out=res[:], in0=live[k, "grad"][:], in1=live[k, "ginv"][:], op=ALU.mult)
             store_tile(*k, res)
 
         def half_finish(*k):
@@ -314,168 +341,184 @@ def tile_diagonalfishernaturalgradient_kernel(tc, x, a, g, w2_bytes, w2_scale, p
                 in_=res[:].rearrange("p (b h) -> p b h", b=n))
 
         ctx.enter_context(tc.manual_schedule())
+        open_dq(0)
         cast_w(0, nc.scalar.copy)
         cast_w(1, nc.vector.tensor_copy)
         finish_factors()
         make_diag(0)
-        tanh(0, 0, 512)
-        sech(0, 0)
         turn_w(0)
         scale_w(0)
         turn_w(1)
         scale_w(1)
         turn_w(2)
+        tanh(0, 0)
+        scale_x(0, 1, nc.vector)
+        make_diag(1)
         turn_w(3)
+        tanh(0, 2)
+        sech(0, 0, 2)
         scale_w(2)
         scale_w(3)
-        tanh(0, 512, 1024)
-        scale_x(0)
-        quant_w(0)
-        turn_g(0, 0)
-        weave_g(0, 0, nc.scalar.copy)
         turn_g(0, 1)
+        turn_g(0, 0)
         weave_g(0, 1, nc.vector.tensor_copy)
-        mul_x2(0, 0)
-        square_x2(0, 0)
-        weave_xp(0, 0)
-        quant_w(1)
-        weave_xp(1, 0)
-        turn_g(1, 0)
         turn_g(1, 1)
-        weave_g(1, 0, nc.scalar.copy)
-        weave_g(1, 1, nc.vector.tensor_copy)
-        scale_x(1)
-        tanh(1, 0, 512)
-        sech(0, 1)
+        weave_g(0, 0, nc.scalar.copy)
+        quant_w(0)
+        turn_g(1, 0)
+        scale_x(0, 3, nc.vector)
+        scale_x(1, 0, nc.gpsimd)
+        scale_x(1, 3, nc.gpsimd)
+        sech(1, 0, 2)
+        scale_x(0, 2, nc.vector)
+        tanh(1, 0)
+        sech(0, 0, 0)
         quant_g(0)
-        weave_xp(0, 1)
-        quant_g(1)
-        weave_xp(1, 1)
-        make_diag(1)
-        mul_x2(0, 1)
-        square_x2(0, 1)
+        sech(0, 1, 0)
         mul_back(0, 0)
+        open_xp(1)
+        quant_w(1)
+        scale_x(0, 0, nc.vector)
+        weave_g(1, 1, nc.vector.tensor_copy)
+        tanh(1, 2)
+        weave_g(1, 0, nc.vector.tensor_copy)
+        sech(1, 0, 0)
         make_e(0, 0)
+        quant_g(1)
+        scale_x(1, 2, nc.vector)
+        scale_x(1, 1, nc.vector)
+        open_xp(0)
+        weave_xp(0, 0)
+        sech(0, 1, 2)
+        weave_xp(0, 1)
+        g_weave_xp(1, 1)
+        mul_back(0, 1)
+        square_d(0, 0)
+        make_e(0, 1)
+        sech(1, 1, 2)
+        square_d(0, 1)
+        weave_dq(0, 0)
+        mul_x2(0, 0)
+        weave_dq(0, 1)
+        mul_x2(0, 1)
+        square_x2(0, 0)
+        square_x2(0, 1)
+        sech(1, 1, 0)
+        g_weave_xp(1, 0)
+        mul_back(1, 0)
+        make_e(1, 0)
+        quant_xp(1)
+        open_dq(1)
+        quant_d2(0)
+        quant_x2(0)
+        square_d(1, 0)
+        open_dq(2)
         mul_x2(1, 0)
         square_x2(1, 0)
+        mul_back(1, 1)
+        make_e(1, 1)
+        mul_fish(0, 0, 0)
+        root(0, 0, 0)
+        mul_fish(0, 0, 3)
         mul_x2(1, 1)
         square_x2(1, 1)
-        quant_xp(0)
-        quant_xp(1)
-        tanh(1, 512, 1024)
-        quant_x2(0)
-        mul_back(0, 1)
-        mul_back(1, 0)
-        make_e(0, 1)
-        square_d(0, 0)
-        square_d(0, 1)
-        quant_x2(1)
-        mul_back(1, 1)
-        weave_dq(0, 0)
-        weave_dq(0, 1)
-        sech(1, 0)
-        make_e(1, 0)
-        quant_d2(0)
-        sech(1, 1)
-        make_e(1, 1)
-        mul_x2(2, 0)
-        square_x2(2, 0)
-        weave_dq(1, 0)
-        weave_dq(1, 1)
-        square_d(1, 0)
-        square_d(1, 1)
-        mul_x2(2, 1)
-        mul_fish(0, 0, 3)
-        root(0, 0, 3)
-        divide(0, 0, 3)
-        mul_fish(0, 0, 1)
-        root(0, 0, 1)
         quant_dq(0)
-        mul_grad(0, 0, 0)
-        mul_fish(0, 0, 0)
-        quant_d2(1)
+        mul_x2(2, 0)
+        mul_fish(0, 0, 1)
+        quant_xp(0)
         mul_grad(0, 0, 3)
-        square_x2(2, 1)
-        weave_dq(2, 0)
-        weave_dq(2, 1)
-        square_d(2, 0)
-        quant_dq(1)
-        mul_fish(0, 0, 2)
-        finish(0, 0, 3)
-        mul_fish(0, 1, 2)
-        mul_grad(0, 0, 2)
-        mul_fish(1, 0, 1)
-        mul_fish(1, 0, 0)
-        root(0, 0, 2)
-        half_finish(0, 0, 2)
-        root(0, 0, 0)
-        half_finish(0, 0, 0)
-        rest_finish(0, 0, 2)
-        square_d(2, 1)
-        quant_d2(2)
-        root(0, 1, 2)
-        mul_grad(0, 1, 2)
-        divide(0, 0, 1)
-        mul_grad(1, 0, 0)
-        mul_grad(1, 1, 0)
-        half_finish(0, 1, 2)
-        quant_dq(2)
-        root(1, 0, 1)
-        mul_fish(0, 1, 0)
-        rest_finish(0, 1, 2)
-        mul_fish(1, 1, 0)
-        rest_finish(0, 0, 0)
+        weave_dq(1, 1)
         mul_grad(0, 0, 1)
-        finish(0, 0, 1)
-        root(1, 0, 0)
-        divide(1, 0, 0)
-        finish(1, 0, 0)
+        g_weave_dq(1, 0)
+        square_d(1, 1)
+        quant_d2(1)
+        root(0, 0, 3)
+        quant_x2(1)
+        quant_dq(1)
+        open_xp(2)
+        root(0, 0, 1)
+        half_finish(0, 0, 1)
+        divide(0, 0, 0)
+        mul_fish(0, 1, 0)
         root(0, 1, 0)
-        divide(0, 1, 0)
+        square_x2(2, 0)
+        half_finish(0, 0, 3)
+        square_d(2, 0)
+        mul_grad(0, 0, 0)
+        finish(0, 0, 0)
+        weave_dq(2, 1)
+        rest_finish(0, 0, 3)
         mul_grad(0, 1, 0)
-        quant_x2(2)
-        weave_xp(2, 0)
-        mul_fish(0, 2, 0)
-        mul_grad(1, 0, 1)
+        square_d(2, 1)
+        rest_finish(0, 0, 1)
+        mul_fish(1, 1, 0)
         root(1, 1, 0)
+        g_divide(0, 1, 0)
+        quant_d2(2)
+        g_finish(0, 1, 0)
+        mul_fish(1, 0, 0)
+        mul_grad(1, 0, 0)
+        root(1, 0, 0)
+        half_finish(1, 0, 0)
+        divide(1, 1, 0)
+        mul_grad(0, 1, 2)
+        mul_grad(1, 1, 0)
+        mul_fish(0, 1, 2)
+        root(0, 1, 2)
+        mul_x2(2, 1)
+        finish(1, 1, 0)
+        mul_fish(1, 0, 1)
+        g_weave_dq(2, 0)
+        half_finish(0, 1, 2)
+        rest_finish(1, 0, 0)
         mul_fish(1, 2, 0)
-        half_finish(1, 1, 0)
-        finish(0, 1, 0)
+        rest_finish(0, 1, 2)
+        square_x2(2, 1)
+        quant_x2(2)
         mul_fish(0, 2, 2)
-        mul_grad(0, 2, 2)
+        root(1, 0, 1)
+        root(1, 2, 0)
+        quant_dq(2)
+        g_divide(1, 2, 0)
+        mul_grad(1, 0, 1)
         divide(1, 0, 1)
         finish(1, 0, 1)
-        root(1, 2, 0)
+        mul_fish(0, 2, 0)
+        s_weave_xp(2, 1)
+        weave_xp(2, 0)
+        mul_fish(0, 0, 2)
         root(0, 2, 0)
-        divide(1, 2, 0)
-        rest_finish(1, 1, 0)
         root(0, 2, 2)
-        weave_xp(2, 1)
-        mul_grad(1, 2, 0)
-        finish(1, 2, 0)
-        half_finish(0, 2, 2)
-        divide(0, 2, 0)
-        quant_xp(2)
-        mul_fish(2, 0, 0)
-        root(2, 0, 0)
-        mul_fish(2, 0, 1)
-        root(2, 0, 1)
-        mul_fish(2, 2, 0)
-        mul_grad(0, 2, 0)
+        root(0, 0, 2)
         mul_fish(2, 1, 0)
-        finish(0, 2, 0)
-        mul_grad(2, 0, 0)
+        mul_grad(0, 0, 2)
+        quant_xp(2)
+        mul_fish(2, 0, 1)
+        divide(0, 2, 2)
+        mul_grad(1, 2, 0)
+        g_finish(1, 2, 0)
+        divide(0, 0, 2)
+        mul_grad(0, 2, 2)
+        mul_grad(0, 2, 0)
+        g_divide(0, 2, 0)
         mul_grad(2, 0, 1)
-        rest_finish(0, 2, 2)
-        divide(2, 0, 0)
-        root(2, 2, 0)
-        finish(2, 0, 0)
-        divide(2, 2, 0)
-        mul_grad(2, 1, 0)
-        half_finish(2, 0, 1)
-        rest_finish(2, 0, 1)
         root(2, 1, 0)
+        root(2, 0, 1)
+        mul_grad(2, 1, 0)
+        g_divide(2, 0, 1)
+        finish(0, 2, 2)
+        mul_fish(2, 2, 0)
         divide(2, 1, 0)
+        finish(0, 0, 2)
+        root(2, 2, 0)
+        mul_fish(2, 0, 0)
+        g_finish(0, 2, 0)
+        root(2, 0, 0)
         finish(2, 1, 0)
+        mul_grad(2, 0, 0)
+        g_finish(2, 0, 1)
+        divide(2, 0, 0)
         mul_grad(2, 2, 0)
-        finish(2, 2, 0)
+        finish(2, 0, 0)
+        g_divide(2, 2, 0)
+        g_finish(2, 2, 0)

@@ -5,6 +5,7 @@ from concourse.masks import make_identity
 
 N, D, H, O = 1024, 1024, 1024, 512
 FLOPS = 2 * N * H * O + 2 * 2 * N * D * H
+DAMP = 0.2
 
 F32 = mybir.dt.float32
 BF16 = mybir.dt.bfloat16
@@ -17,9 +18,11 @@ ACT = mybir.ActivationFunctionType
 
 P = 128
 T = 4
-G = 2
-D_CHUNKS = ((0, 512), (512, 256), (768, 256))
-X_CHUNKS = ((0, 512), (512, 256), (768, 256))
+G = N // (P * T)
+HALF = 512
+M = HALF // P
+RUN = 4
+TINY = 2.0**-100
 
 
 def tile_diagonalfishernaturalgradient_kernel(tc, x, a, g, w2_bytes, w2_scale, p, q, s, out):
@@ -29,39 +32,43 @@ def tile_diagonalfishernaturalgradient_kernel(tc, x, a, g, w2_bytes, w2_scale, p
         stage = ctx.enter_context(tc.tile_pool(name="stage", bufs=2))
         psum = ctx.enter_context(tc.psum_pool(name="psum", bufs=8))
 
-        def bank_tile():
-            return psum.tile([P, 512], F32, name="bank")
+        def new_bank():
+            return psum.tile([P, HALF], F32, name="bank")
 
-        pqs_raw = keep.tile([P, 3, 2 * G * T], BF16, name="pqs_raw")
-        for i, v in enumerate((p, q, s)):
-            nc.scalar.dma_start(out=pqs_raw[:, i, 0:G * T].rearrange("p (g t) -> p g t", t=T), in_=v.rearrange("(g p t) -> p g t", p=P, t=T))
+        gains = keep.tile([P, 3, 16], BF16, name="gains")
+        for n, vector in enumerate((p, q, s)):
+            nc.scalar.dma_start(
+                out=gains[:, n, 0 : G * T].rearrange("p (i t) -> p i t", t=T),
+                in_=vector.rearrange("(i p t) -> p i t", p=P, t=T),
+            )
         w_scale = keep.tile([P, T], F32, name="w_scale")
         nc.scalar.dma_start(out=w_scale[:], in_=w2_scale.rearrange("o (p t) -> p (o t)", t=T))
-        w_raw = keep.tile([P, 8 * O], U8, name="w_raw")
-        w_view = w2_bytes.rearrange("(r p) k -> p r k", p=P)
-        g_view = g.rearrange("(g p t) k -> g p t k", p=P, t=T)
-        a_view = a.rearrange("(g p t) k -> g p t k", p=P, t=T)
-        x_view = x.rearrange("(g p t) k -> g p t k", p=P, t=T)
-        g_raw = [keep.tile([P, T, O], BF16, name="g_raw%d" % i) for i in range(G)]
-        a_raw = [keep.tile([P, T, H], BF16, name="a_raw%d" % i) for i in range(G)]
-        x_raw = [keep.tile([P, T, D], BF16, name="x_raw%d" % i) for i in range(G)]
 
-        def load_w(i):
-            nc.sync.dma_start(out=w_raw[:, i * 2048:(i + 1) * 2048].rearrange("p (r k) -> p r k", k=O), in_=w_view[:, 4 * i:4 * i + 4, :])
+        w_bytes = [keep.tile([P, M * O], U8, name="w_bytes%d" % hh) for hh in range(2)]
+        g_rows = [keep.tile([P, T, O], BF16, name="g_rows%d" % i) for i in range(G)]
+        a_rows = [keep.tile([P, T, H], BF16, name="a_rows%d" % i) for i in range(G)]
+        x_rows = [keep.tile([P, T, D], BF16, name="x_rows%d" % i) for i in range(G)]
 
-        def load(tiles, view, i, t0, t1):
-            nc.sync.dma_start(out=tiles[i][:, t0:t1], in_=view[i][:, t0:t1])
+        def load_w(hh):
+            nc.sync.dma_start(
+                out=w_bytes[hh][:].rearrange("p (r k) -> p r k", k=O),
+                in_=w2_bytes.rearrange("(hh r p) k -> hh p r k", hh=2, p=P)[hh],
+            )
+
+        def load(tiles, tensor, i, t0, t1):
+            rows = tensor.rearrange("(i p t) c -> i p t c", p=P, t=T)[i]
+            nc.sync.dma_start(out=tiles[i][:, t0:t1], in_=rows[:, t0:t1])
 
         load_w(0)
         load_w(1)
-        load(a_raw, a_view, 0, 0, 2)
-        load(x_raw, x_view, 0, 0, 2)
-        load(a_raw, a_view, 0, 2, 4)
-        load(g_raw, g_view, 0, 0, 4)
-        load(x_raw, x_view, 0, 2, 4)
-        load(a_raw, a_view, 1, 0, 4)
-        load(g_raw, g_view, 1, 0, 4)
-        load(x_raw, x_view, 1, 0, 4)
+        load(a_rows, a, 0, 0, 2)
+        load(x_rows, x, 0, 0, 2)
+        load(a_rows, a, 0, 2, 4)
+        load(g_rows, g, 0, 0, 4)
+        load(x_rows, x, 0, 2, 4)
+        load(a_rows, a, 1, 0, 4)
+        load(g_rows, g, 1, 0, 4)
+        load(x_rows, x, 1, 0, 4)
 
         warm = keep.tile([P, 1], F32, name="warm")
         nc.vector.memset(warm[:], 0.0)
@@ -71,454 +78,318 @@ def tile_diagonalfishernaturalgradient_kernel(tc, x, a, g, w2_bytes, w2_scale, p
         ident_bf = keep.tile([P, P], BF16, name="ident_bf")
         nc.vector.tensor_copy(out=ident_bf[:], in_=ident[:])
 
-        quarter = keep.tile([P, 2 * G * T], F32, name="quarter")
+        quarter = keep.tile([P, 2, G * T], F32, name="quarter")
         nc.gpsimd.memset(quarter[:], 0.25)
         pqs = keep.tile([P, 3, G * T], F32, name="pqs")
-        nc.vector.tensor_copy(out=pqs[:], in_=pqs_raw[:, :, 0:G * T])
+        nc.vector.tensor_copy(out=pqs[:], in_=gains[:, :, 0 : G * T])
         weight = keep.tile([P, 2, G * T], F32, name="weight")
         nc.vector.tensor_tensor(out=weight[:], in0=pqs[:, 0:2, :], in1=pqs[:, 2:3, :].to_broadcast([P, 2, G * T]), op=ALU.mult)
-        magnitude = keep.tile([P, 2, G * T], F32, name="magnitude")
-        nc.vector.scalar_tensor_tensor(out=magnitude[:], in0=weight[:], scalar=-1.0, in1=weight[:], op0=ALU.mult, op1=ALU.max)
-        nc.vector.tensor_scalar(out=magnitude[:], in0=magnitude[:], scalar1=2.0 ** -100, scalar2=None, op0=ALU.max)
+        size = keep.tile([P, 2, G * T], F32, name="size")
+        nc.vector.scalar_tensor_tensor(out=size[:], in0=weight[:], scalar=-1.0, in1=weight[:], op0=ALU.mult, op1=ALU.max)
+        nc.vector.tensor_scalar(out=size[:], in0=size[:], scalar1=TINY, scalar2=None, op0=ALU.max)
         root4 = keep.tile([P, 2, G * T], F32, name="root4")
-        nc.gpsimd.tensor_tensor(out=root4[:].rearrange("p a j -> p (a j)"), in0=magnitude[:].rearrange("p a j -> p (a j)"), in1=quarter[:], op=ALU.pow)
+        nc.gpsimd.tensor_tensor(
+            out=root4[:].rearrange("p a j -> p (a j)"), in0=size[:].rearrange("p a j -> p (a j)"),
+            in1=quarter[:].rearrange("p a j -> p (a j)"), op=ALU.pow,
+        )
         root2 = keep.tile([P, 2, G * T], F32, name="root2")
-        f_inv = keep.tile([P, G * T], F32, name="f_inv")
-        neg_c = keep.tile([P, G * T], F32, name="neg_c")
-        r_hi = keep.tile([P, G * T], BF16, name="r_hi")
-        r_lo = keep.tile([P, G * T], F32, name="r_lo")
+        r_head = keep.tile([P, G * T], BF16, name="r_head")
+        r_tail = keep.tile([P, G * T], F32, name="r_tail")
+        f_inverse = keep.tile([P, G * T], F32, name="f_inverse")
+        ratio = keep.tile([P, G * T], F32, name="ratio")
 
         def finish_factors():
-            nc.vector.tensor_tensor(out=root2[:], in0=root4[:], in1=root4[:], op=ALU.mult)
-            nc.vector.reciprocal(out=f_inv[:], in_=root2[:, 1, :])
-            nc.vector.tensor_copy(out=r_hi[:], in_=root2[:, 0, :])
-            nc.vector.scalar_tensor_tensor(out=neg_c[:], in0=f_inv[:], scalar=-1.0, in1=pqs[:, 1, :], op0=ALU.mult, op1=ALU.mult)
-            nc.vector.tensor_tensor(out=r_lo[:], in0=root2[:, 0, :], in1=r_hi[:], op=ALU.subtract)
+            nc.gpsimd.tensor_tensor(out=root2[:], in0=root4[:], in1=root4[:], op=ALU.mult)
+            nc.gpsimd.tensor_copy(out=r_head[:], in_=root2[:, 0, :])
+            nc.gpsimd.tensor_tensor(out=r_tail[:], in0=root2[:, 0, :], in1=r_head[:], op=ALU.subtract)
+            nc.vector.reciprocal(out=f_inverse[:], in_=root2[:, 1, :])
+            nc.vector.scalar_tensor_tensor(out=ratio[:], in0=f_inverse[:], scalar=-1.0, in1=pqs[:, 1, :], op0=ALU.mult, op1=ALU.mult)
 
         diag = keep.tile([P, 2, G * T, P], BF16, name="diag")
 
         def make_diag(i):
             js = slice(i * T, (i + 1) * T)
-            for k, r in enumerate((root2[:, 0, js], r_lo[:, js])):
-                nc.gpsimd.tensor_tensor(out=diag[:, k, js, :], in0=ident_bf[:].unsqueeze(1).to_broadcast([P, T, P]), in1=r.unsqueeze(2).to_broadcast([P, T, P]), op=ALU.mult)
+            for n, part in enumerate((root2[:, 0, js], r_tail[:, js])):
+                nc.gpsimd.tensor_tensor(
+                    out=diag[:, n, js, :], in0=ident_bf[:].unsqueeze(1).to_broadcast([P, T, P]),
+                    in1=part.unsqueeze(2).to_broadcast([P, T, P]), op=ALU.mult,
+                )
 
-        w_wide = keep.tile([P, 8 * O], BF16, name="w_wide")
+        def turn(bank, rows_bf16, col, stride):
+            words = rows_bf16.bitcast(F32)
+            for u in range(2):
+                nc.tensor.transpose(bank[:, col + u * stride : col + u * stride + P], words[:, u::2], ident[:])
+
+        w_wide = [keep.tile([P, M * O], BF16, name="w_wide%d" % hh) for hh in range(2)]
         w_codes = keep.tile([P, H], U32, name="w_codes", align_bytes=64)
         w_scales = keep.tile([P, H], U8, name="w_scales", align_bytes=64)
-        scale_pair = w_scale[:].rearrange("p (u e) -> p u e", e=2).unsqueeze(1).to_broadcast([P, 256, 2, 2])
-        w_il = {}
+        scale_of_k = w_scale[:].rearrange("p (u e) -> p u e", e=2).unsqueeze(1).to_broadcast([P, 2 * P, 2, 2])
+        w_banks, w_woven = {}, {}
 
         def cast_w(hh, copy):
-            half = slice(hh * 2048, (hh + 1) * 2048)
-            copy(out=w_wide[:, half], in_=w_raw[:, half].bitcast(FP8))
+            copy(out=w_wide[hh][:], in_=w_bytes[hh][:].bitcast(FP8))
 
-        w_banks = {}
+        def turn_w(hh, b):
+            w_banks[hh, b] = new_bank()
+            for n in range(2):
+                r = 2 * b + n
+                turn(w_banks[hh, b], w_wide[hh][:, r * O : (r + 1) * O], n * P, 2 * P)
 
-        def turn_w(b):
-            bank = bank_tile()
-            w_banks[b] = bank
-            for rr in range(2):
-                r = 2 * b + rr
-                words = w_wide[:, r * O:(r + 1) * O].bitcast(F32)
-                for u in range(2):
-                    nc.tensor.transpose(bank[:, u * 256 + rr * P:u * 256 + (rr + 1) * P], words[:, u::2], ident[:])
-
-        def scale_w(b):
-            if b % 2 == 0:
-                w_il[b // 2] = stage.tile([P, 512, T], BF16, name="w_il", tag="head_il", bufs=3, align_bytes=64)
+        def scale_w(hh, b):
+            if b == 0:
+                w_woven[hh] = stage.tile([P, HALF, T], BF16, name="w_woven", tag="turned", bufs=3, align_bytes=64)
             nc.vector.tensor_tensor(
-                out=w_il[b // 2][:, (b % 2) * 256:(b % 2 + 1) * 256, :].rearrange("p h (u e) -> p h u e", e=2),
-                in0=w_banks[b][:].bitcast(BF16).rearrange("p (u h e) -> p h u e", u=2, e=2),
-                in1=scale_pair, op=ALU.mult)
+                out=w_woven[hh][:, b * 2 * P : (b + 1) * 2 * P, :].rearrange("p h (u e) -> p h u e", e=2),
+                in0=scale_of_k,
+                in1=w_banks[hh, b][:].bitcast(BF16).rearrange("p (u h e) -> p h u e", u=2, e=2),
+                op=ALU.mult,
+            )
 
         def quant_w(hh):
-            cols = slice(hh * 512, (hh + 1) * 512)
-            nc.vector.quantize_mx(out=w_codes[:, cols].bitcast(FP8X4), scales=w_scales[:, cols], in_=w_il[hh][:].rearrange("p h t -> p (h t)"))
+            cols = slice(hh * HALF, (hh + 1) * HALF)
+            nc.vector.quantize_mx(
+                out=w_codes[:, cols].bitcast(FP8X4), scales=w_scales[:, cols], in_=w_woven[hh][:].rearrange("p h t -> p (h t)")
+            )
 
-        g_codes = keep.tile([P, G, 512], U32, name="g_codes", align_bytes=64)
-        g_scales = keep.tile([P, G, 512], U8, name="g_scales", align_bytes=64)
-        g_ils = {}
-
-        g_banks = {}
+        g_codes = keep.tile([P, G, HALF], U32, name="g_codes", align_bytes=64)
+        g_scales = keep.tile([P, G, HALF], U8, name="g_scales", align_bytes=64)
+        g_banks, g_woven = {}, {}
 
         def turn_g(i, b):
-            bank = bank_tile()
-            g_banks[i, b] = bank
-            if b == 0:
-                g_ils[i] = stage.tile([P, T * P, T], BF16, name="g_il", tag="head_il", bufs=3, align_bytes=64)
-            for tt in range(2):
-                words = g_raw[i][:, 2 * b + tt, :].bitcast(F32)
-                for u in range(2):
-                    nc.tensor.transpose(bank[:, (2 * tt + u) * P:(2 * tt + u + 1) * P], words[:, u::2], ident[:])
+            g_banks[i, b] = new_bank()
+            for n in range(2):
+                turn(g_banks[i, b], g_rows[i][:, 2 * b + n, :], n * 2 * P, P)
 
         def weave_g(i, b, copy):
+            if b == 0:
+                g_woven[i] = stage.tile([P, T * P, T], BF16, name="g_woven", tag="turned", bufs=3, align_bytes=64)
+            words = g_woven[i][:, b * 2 * P : (b + 1) * 2 * P, :].rearrange("p n t -> p (n t)").bitcast(F32)
             copy(
-                out=g_ils[i][:, b * 256:(b + 1) * 256, :].rearrange("p n t -> p (n t)").bitcast(F32).rearrange("p (t m u) -> p t m u", t=2, u=2),
-                in_=g_banks[i, b][:].rearrange("p (t u m) -> p t m u", t=2, u=2))
+                out=words.rearrange("p (n m u) -> p n m u", n=2, u=2),
+                in_=g_banks[i, b][:].rearrange("p (n u m) -> p n m u", n=2, u=2),
+            )
 
         def quant_g(i):
-            nc.vector.quantize_mx(out=g_codes[:, i, :].bitcast(FP8X4), scales=g_scales[:, i, :], in_=g_ils[i][:].rearrange("p n t -> p (n t)"))
+            nc.vector.quantize_mx(
+                out=g_codes[:, i, :].bitcast(FP8X4), scales=g_scales[:, i, :], in_=g_woven[i][:].rearrange("p n t -> p (n t)")
+            )
 
-        xp_codes = [keep.tile([P, G, w], U32, name="xp_codes%d" % c0, align_bytes=64) for c0, w in X_CHUNKS]
-        xp_scales = [keep.tile([P, G, w], U8, name="xp_scales%d" % c0, align_bytes=64) for c0, w in X_CHUNKS]
-        x2_codes = [keep.tile([P, G, w], U32, name="x2_codes%d" % c0, align_bytes=64) for c0, w in X_CHUNKS]
-        x2_scales = [keep.tile([P, G, w], U8, name="x2_scales%d" % c0, align_bytes=64) for c0, w in X_CHUNKS]
-        xp_planar = [keep.tile([P, T, D], BF16, name="xp_planar%d" % i) for i in range(G)]
-        xp_ils = {}
-        x2_ils = {}
-        x2_banks = {}
+        def code_tiles(name):
+            codes = [keep.tile([P, G, HALF], U32, name="%s_codes%d" % (name, n), align_bytes=64) for n in range(2)]
+            scales = [keep.tile([P, G, HALF], U8, name="%s_scales%d" % (name, n), align_bytes=64) for n in range(2)]
+            return codes, scales
+
+        def new_woven():
+            return stage.tile([P, G, HALF, T], BF16, name="woven", bufs=5, align_bytes=64)
+
+        def quantize(operand, n, woven):
+            codes, scales = operand
+            nc.vector.quantize_mx(
+                out=codes[n][:].rearrange("p i c -> p (i c)").bitcast(FP8X4),
+                scales=scales[n][:].rearrange("p i c -> p (i c)"),
+                in_=woven[:].rearrange("p i c t -> p (i c t)"),
+            )
+
+        def runs(planes):
+            return planes.rearrange("p t (c e) -> p c t e", e=RUN)
+
+        def woven_runs(woven, i):
+            return woven[:, i].rearrange("p (c e) t -> p c t e", e=RUN)
+
+        xp, x2, dq, d2 = code_tiles("xp"), code_tiles("x2"), code_tiles("dq"), code_tiles("d2")
+        xp_planes = [keep.tile([P, T, D], BF16, name="xp_planes%d" % i) for i in range(G)]
+        xp_woven, x2_woven, x2_banks = {}, {}, {}
 
         def scale_x(i, t, engine):
-            engine.tensor_scalar(out=xp_planar[i][:, t, :], in0=x_raw[i][:, t, :], scalar1=pqs[:, 0, i * T + t:i * T + t + 1], scalar2=0.0, op0=ALU.mult, op1=ALU.add)
-
-        def open_xp(j):
-            xp_ils[j] = stage.tile([P, G, X_CHUNKS[j][1], T], BF16, name="xp_il", tag="il", bufs=5, align_bytes=64)
+            gain = pqs[:, 0, i * T + t : i * T + t + 1]
+            engine.tensor_scalar(out=xp_planes[i][:, t, :], in0=x_rows[i][:, t, :], scalar1=gain, scalar2=0.0, op0=ALU.mult, op1=ALU.add)
 
         def weave_xp(j, i):
-            c0, w = X_CHUNKS[j]
-            nc.vector.tensor_copy(out=xp_ils[j][:, i].rearrange("p (c i) t -> p c t i", i=4), in_=xp_planar[i][:, :, c0:c0 + w].rearrange("p t (c i) -> p c t i", i=4))
-
-        def s_weave_xp(j, i):
-            c0, w = X_CHUNKS[j]
-            nc.scalar.copy(out=xp_ils[j][:, i].rearrange("p (c i) t -> p c t i", i=4), in_=xp_planar[i][:, :, c0:c0 + w].rearrange("p t (c i) -> p c t i", i=4))
-
-        def g_weave_xp(j, i):
-            c0, w = X_CHUNKS[j]
-            nc.gpsimd.tensor_scalar(out=xp_ils[j][:, i], in0=xp_planar[i][:, :, c0:c0 + w].rearrange("p t c -> p c t"), scalar1=1.0, scalar2=0.0, op0=ALU.mult, op1=ALU.add)
-
-        def quantize(codes, scales, j, il):
-            nc.vector.quantize_mx(
-                out=codes[j][:].rearrange("p g c -> p (g c)").bitcast(FP8X4),
-                scales=scales[j][:].rearrange("p g c -> p (g c)"),
-                in_=il[:].rearrange("p g c t -> p (g c t)"))
-
-        def quant_xp(j):
-            quantize(xp_codes, xp_scales, j, xp_ils[j])
+            nc.vector.tensor_copy(out=woven_runs(xp_woven[j], i), in_=runs(xp_planes[i][:, :, j * HALF : (j + 1) * HALF]))
 
         def mul_x2(j, i):
-            c0, w = X_CHUNKS[j]
-            for b in range(w // P):
-                bank = bank_tile()
-                x2_banks[j, i, b] = bank
-                cols = slice(c0 + b * P, c0 + (b + 1) * P)
+            for b in range(M):
+                x2_banks[j, i, b] = new_bank()
+                cols = slice(j * HALF + b * P, j * HALF + (b + 1) * P)
                 for t in range(T):
-                    for k in range(2):
-                        nc.tensor.matmul(bank[:, t * P:(t + 1) * P], lhsT=diag[:, k, i * T + t, :], rhs=x_raw[i][:, t, cols], start=(k == 0), stop=(k == 1))
+                    for n in range(2):
+                        nc.tensor.matmul(
+                            x2_banks[j, i, b][:, t * P : (t + 1) * P], lhsT=diag[:, n, i * T + t, :], rhs=x_rows[i][:, t, cols],
+                            start=(n == 0), stop=(n == 1),
+                        )
 
         def square_x2(j, i):
-            c0, w = X_CHUNKS[j]
             if i == 0:
-                x2_ils[j] = stage.tile([P, G, w, T], BF16, name="x2_il", tag="il", bufs=5, align_bytes=64)
-            for b in range(w // P):
-                nc.scalar.activation(out=x2_ils[j][:, i, b * P:(b + 1) * P, :], in_=x2_banks[j, i, b][:].rearrange("p (t d) -> p d t", t=T), func=ACT.Square)
+                x2_woven[j] = new_woven()
+            for b in range(M):
+                nc.scalar.activation(
+                    out=x2_woven[j][:, i, b * P : (b + 1) * P, :], in_=x2_banks[j, i, b][:].rearrange("p (t c) -> p c t", t=T), func=ACT.Square
+                )
 
-        def quant_x2(j):
-            quantize(x2_codes, x2_scales, j, x2_ils[j])
-
-        dq_codes = [keep.tile([P, G, w], U32, name="dq_codes%d" % c0, align_bytes=64) for c0, w in D_CHUNKS]
-        dq_scales = [keep.tile([P, G, w], U8, name="dq_scales%d" % c0, align_bytes=64) for c0, w in D_CHUNKS]
-        d2_codes = [keep.tile([P, G, w], U32, name="d2_codes%d" % c0, align_bytes=64) for c0, w in D_CHUNKS]
-        d2_scales = [keep.tile([P, G, w], U8, name="d2_scales%d" % c0, align_bytes=64) for c0, w in D_CHUNKS]
-        th = [keep.tile([P, T, H], F32, name="th%d" % i) for i in range(G)]
-        back_banks = {}
-        dq_ils = {}
-        d2_ils = {}
+        d_planes = [keep.tile([P, T, H], F32, name="d_planes%d" % i) for i in range(G)]
+        back_banks, dq_woven, d2_woven = {}, {}, {}
 
         def tanh(i, t0):
-            nc.scalar.activation(out=th[i][:, t0:t0 + 2], in_=a_raw[i][:, t0:t0 + 2], func=ACT.Tanh)
+            nc.scalar.activation(out=d_planes[i][:, t0 : t0 + 2], in_=a_rows[i][:, t0 : t0 + 2], func=ACT.Tanh)
 
-        def sech(hh, i, t0):
+        def square_tanh(i, t0, c0, c1):
             for t in range(t0, t0 + 2):
-                j = i * T + t
-                sq = th[i][:, t, hh * 512:(hh + 1) * 512]
-                nc.scalar.activation(out=sq, in_=sq, func=ACT.Square, scale=root4[:, 1, j:j + 1])
+                plane = d_planes[i][:, t, c0:c1]
+                nc.scalar.activation(out=plane, in_=plane, func=ACT.Square, scale=root4[:, 1, i * T + t : i * T + t + 1])
 
         def mul_back(hh, i):
-            cols = slice(hh * 512, (hh + 1) * 512)
+            cols = slice(hh * HALF, (hh + 1) * HALF)
             for t in range(T):
-                bank = bank_tile()
-                back_banks[hh, i, t] = bank
+                back_banks[hh, i, t] = new_bank()
                 rows = slice(t * P, (t + 1) * P)
                 nc.tensor.matmul_mx(
-                    out=bank[:], lhsT=g_codes[:, i, rows].bitcast(FP8X4), lhsT_scale=g_scales[:, i, rows],
-                    rhs=w_codes[:, cols].bitcast(FP8X4), rhs_scale=w_scales[:, cols], start=True, stop=True)
+                    out=back_banks[hh, i, t][:], lhsT=g_codes[:, i, rows].bitcast(FP8X4), lhsT_scale=g_scales[:, i, rows],
+                    rhs=w_codes[:, cols].bitcast(FP8X4), rhs_scale=w_scales[:, cols], start=True, stop=True,
+                )
 
-        def make_e(hh, i):
+        def make_d(hh, i):
             for t in range(T):
-                j = i * T + t
-                e = th[i][:, t, hh * 512:(hh + 1) * 512]
-                nc.vector.scalar_tensor_tensor(out=e, in0=e, scalar=root2[:, 1, j:j + 1], in1=back_banks[hh, i, t][:], op0=ALU.subtract, op1=ALU.mult)
+                plane = d_planes[i][:, t, hh * HALF : (hh + 1) * HALF]
+                f = root2[:, 1, i * T + t : i * T + t + 1]
+                nc.vector.scalar_tensor_tensor(out=plane, in0=plane, scalar=f, in1=back_banks[hh, i, t][:], op0=ALU.subtract, op1=ALU.mult)
 
-        def square_d(c, i):
-            c0, w = D_CHUNKS[c]
+        def weave_dq(hh, i):
+            factor = ratio[:, i * T : (i + 1) * T].unsqueeze(1).unsqueeze(3).to_broadcast([P, HALF // RUN, T, RUN])
+            nc.vector.tensor_tensor(
+                out=woven_runs(dq_woven[hh], i), in0=runs(d_planes[i][:, :, hh * HALF : (hh + 1) * HALF]), in1=factor, op=ALU.mult
+            )
+
+        def square_d2(hh, i):
             if i == 0:
-                d2_ils[c] = stage.tile([P, G, w, T], BF16, name="d2_il", tag="il", bufs=5, align_bytes=64)
-            e = th[i][:, :, c0:c0 + w].rearrange("p t (c i) -> p c t i", i=4)
-            nc.scalar.activation(out=d2_ils[c][:, i].rearrange("p (c i) t -> p c t i", i=4), in_=e, func=ACT.Square)
+                d2_woven[hh] = new_woven()
+            nc.scalar.activation(out=woven_runs(d2_woven[hh], i), in_=runs(d_planes[i][:, :, hh * HALF : (hh + 1) * HALF]), func=ACT.Square)
 
-        def open_dq(c):
-            dq_ils[c] = stage.tile([P, G, D_CHUNKS[c][1], T], BF16, name="dq_il", tag="il", bufs=5, align_bytes=64)
+        tiles = [(j, hh, m) for j in range(2) for hh in range(2) for m in range(M)]
+        fish_bank, grad_bank, root_of, inverse_of = {}, {}, {}, {}
 
-        def g_weave_dq(c, i):
-            c0, w = D_CHUNKS[c]
-            e = th[i][:, :, c0:c0 + w].rearrange("p t c -> p c t")
-            factor = neg_c[:, i * T:(i + 1) * T].unsqueeze(1).to_broadcast([P, w, T])
-            nc.gpsimd.tensor_tensor(out=dq_ils[c][:, i], in0=e, in1=factor, op=ALU.mult)
-
-        def weave_dq(c, i):
-            c0, w = D_CHUNKS[c]
-            e = th[i][:, :, c0:c0 + w].rearrange("p t (c i) -> p c t i", i=4)
-            factor = neg_c[:, i * T:(i + 1) * T].unsqueeze(1).unsqueeze(3).to_broadcast([P, w // 4, T, 4])
-            nc.vector.tensor_tensor(out=dq_ils[c][:, i].rearrange("p (c i) t -> p c t i", i=4), in0=e, in1=factor, op=ALU.mult)
-
-        def quant_d2(c):
-            quantize(d2_codes, d2_scales, c, d2_ils[c])
-
-        def quant_dq(c):
-            quantize(dq_codes, dq_scales, c, dq_ils[c])
-
-        live = {}
-
-        def product(j, c, m, lc, ls, rc, rs):
-            w = D_CHUNKS[c][1]
-            bank = bank_tile()
-            for b in range(512 // w):
-                rows = slice((m + b) * P, (m + b + 1) * P)
-                for i in range(G):
-                    nc.tensor.matmul_mx(
-                        out=bank[:, b * w:(b + 1) * w], lhsT=lc[j][:, i, rows].bitcast(FP8X4), lhsT_scale=ls[j][:, i, rows],
-                        rhs=rc[c][:, i, :].bitcast(FP8X4), rhs_scale=rs[c][:, i, :], start=(i == 0), stop=(i == G - 1))
+        def product(k, lhs, rhs):
+            j, hh, m = tiles[k]
+            bank = new_bank()
+            rows = slice(m * P, (m + 1) * P)
+            for i in range(G):
+                nc.tensor.matmul_mx(
+                    out=bank[:], lhsT=lhs[0][j][:, i, rows].bitcast(FP8X4), lhsT_scale=lhs[1][j][:, i, rows],
+                    rhs=rhs[0][hh][:, i, :].bitcast(FP8X4), rhs_scale=rhs[1][hh][:, i, :], start=(i == 0), stop=(i == G - 1),
+                )
             return bank
 
-        def mul_fish(*k):
-            live[k, "fish"] = product(*k, x2_codes, x2_scales, d2_codes, d2_scales)
+        def inverse_root(k):
+            root_of[k] = stage.tile([P, HALF], F32, name="root", bufs=4)
+            nc.scalar.activation(out=root_of[k][:], in_=fish_bank[k][:], func=ACT.Abs_reciprocal_sqrt, scale=1.0 / 32.0, bias=32.0 * DAMP)
 
-        def mul_grad(*k):
-            live[k, "grad"] = product(*k, xp_codes, xp_scales, dq_codes, dq_scales)
-
-        def root(*k):
-            live[k, "root"] = stage.tile([P, 512], F32, name="inv_root", bufs=4)
-            nc.scalar.activation(out=live[k, "root"][:], in_=live[k, "fish"][:], func=ACT.Abs_reciprocal_sqrt, scale=1.0 / 32.0, bias=6.4)
-
-        def divide(*k):
-            live[k, "inv"] = stage.tile([P, 512], F32, name="inv")
-            nc.scalar.activation(out=live[k, "inv"][:], in_=live[k, "root"][:], func=ACT.Square)
-
-        def g_divide(*k):
-            live[k, "ginv"] = stage.tile([P, 512], F32, name="ginv")
-            nc.gpsimd.tensor_tensor(out=live[k, "ginv"][:], in0=live[k, "root"][:], in1=live[k, "root"][:], op=ALU.mult)
-
-        def finish(*k):
-            res = stage.tile([P, 512], F32, name="res", bufs=4)
-            nc.vector.tensor_tensor(out=res[:], in0=live[k, "grad"][:], in1=live[k, "inv"][:], op=ALU.mult)
-            store_tile(*k, res)
-
-        def g_rest_finish(*k):
-            res = stage.tile([P, 512], F32, name="res", bufs=4)
-            nc.gpsimd.tensor_tensor(out=res[:], in0=live[k, "part"][:], in1=live[k, "root"][:], op=ALU.mult)
-            store_tile(*k, res)
-
-        def g_finish(*k):
-            res = stage.tile([P, 512], F32, name="res", bufs=4)
-            nc.vector.tensor_tensor(out=res[:], in0=live[k, "grad"][:], in1=live[k, "ginv"][:], op=ALU.mult)
-            store_tile(*k, res)
-
-        def half_finish(*k):
-            live[k, "part"] = stage.tile([P, 512], F32, name="part")
-            nc.vector.tensor_tensor(out=live[k, "part"][:], in0=live[k, "grad"][:], in1=live[k, "root"][:], op=ALU.mult)
-
-        def rest_finish(*k):
-            res = stage.tile([P, 512], F32, name="res", bufs=4)
-            nc.vector.tensor_tensor(out=res[:], in0=live[k, "part"][:], in1=live[k, "root"][:], op=ALU.mult)
-            store_tile(*k, res)
-
-        def store_tile(j, c, m, res):
-            x0 = X_CHUNKS[j][0] + m * P
-            c0, w = D_CHUNKS[c]
-            n = 512 // w
-            nc.sync.dma_start(
-                out=out[x0:x0 + n * P, c0:c0 + w].rearrange("(b p) h -> p b h", p=P),
-                in_=res[:].rearrange("p (b h) -> p b h", b=n))
+        def finish(k):
+            j, hh, m = tiles[k]
+            if k > 5 and k % 2 == 1:
+                inverse = stage.tile([P, HALF], F32, name="inverse_g")
+                nc.gpsimd.tensor_tensor(out=inverse[:], in0=root_of[k][:], in1=root_of[k][:], op=ALU.mult)
+            else:
+                inverse = stage.tile([P, HALF], F32, name="inverse_s")
+                nc.scalar.activation(out=inverse[:], in_=root_of[k][:], func=ACT.Square)
+            result = stage.tile([P, HALF], F32, name="result", bufs=4)
+            nc.vector.tensor_tensor(out=result[:], in0=inverse[:], in1=grad_bank[k][:], op=ALU.mult)
+            row = j * HALF + m * P
+            nc.sync.dma_start(out=out[row : row + P, hh * HALF : (hh + 1) * HALF], in_=result[:])
 
         ctx.enter_context(tc.manual_schedule())
-        open_dq(0)
-        cast_w(0, nc.scalar.copy)
-        cast_w(1, nc.vector.tensor_copy)
+        on_scalar, on_vector = nc.scalar.copy, nc.vector.tensor_copy
+
+        cast_w(0, on_scalar)
+        cast_w(1, on_vector)
         finish_factors()
+        xp_woven[0] = new_woven()
+        turn_w(0, 0)
+        scale_w(0, 0)
         make_diag(0)
-        turn_w(0)
-        scale_w(0)
-        turn_w(1)
-        scale_w(1)
-        turn_w(2)
+        turn_w(0, 1)
+        scale_w(0, 1)
         tanh(0, 0)
-        scale_x(0, 1, nc.vector)
-        make_diag(1)
-        turn_w(3)
+        turn_w(1, 0)
+        scale_w(1, 0)
         tanh(0, 2)
-        sech(0, 0, 2)
-        scale_w(2)
-        scale_w(3)
-        turn_g(0, 1)
-        turn_g(0, 0)
-        weave_g(0, 1, nc.vector.tensor_copy)
-        turn_g(1, 1)
-        weave_g(0, 0, nc.scalar.copy)
+        turn_w(1, 1)
+        for t in range(T):
+            scale_x(0, t, nc.vector)
+        square_tanh(0, 0, 0, HALF)
         quant_w(0)
-        turn_g(1, 0)
-        scale_x(0, 3, nc.vector)
-        scale_x(1, 0, nc.gpsimd)
-        scale_x(1, 3, nc.gpsimd)
-        sech(1, 0, 2)
-        scale_x(0, 2, nc.vector)
-        tanh(1, 0)
-        sech(0, 0, 0)
-        quant_g(0)
-        sech(0, 1, 0)
-        mul_back(0, 0)
-        open_xp(1)
-        quant_w(1)
-        scale_x(0, 0, nc.vector)
-        weave_g(1, 1, nc.vector.tensor_copy)
-        tanh(1, 2)
-        weave_g(1, 0, nc.vector.tensor_copy)
-        sech(1, 0, 0)
-        make_e(0, 0)
-        quant_g(1)
-        scale_x(1, 2, nc.vector)
-        scale_x(1, 1, nc.vector)
-        open_xp(0)
-        weave_xp(0, 0)
-        sech(0, 1, 2)
-        weave_xp(0, 1)
-        g_weave_xp(1, 1)
-        mul_back(0, 1)
-        square_d(0, 0)
-        make_e(0, 1)
-        sech(1, 1, 2)
-        square_d(0, 1)
-        weave_dq(0, 0)
+        turn_g(0, 0)
+        turn_g(0, 1)
+        weave_g(0, 0, on_vector)
+        weave_g(0, 1, on_scalar)
+        square_tanh(0, 2, 0, HALF)
+        square_tanh(0, 0, HALF, H)
         mul_x2(0, 0)
-        weave_dq(0, 1)
-        mul_x2(0, 1)
+        scale_w(1, 1)
+        quant_g(0)
+        quant_w(1)
         square_x2(0, 0)
-        square_x2(0, 1)
-        sech(1, 1, 0)
-        g_weave_xp(1, 0)
+        square_tanh(0, 2, HALF, H)
+        mul_back(0, 0)
         mul_back(1, 0)
-        make_e(1, 0)
-        quant_xp(1)
-        open_dq(1)
-        quant_d2(0)
-        quant_x2(0)
-        square_d(1, 0)
-        open_dq(2)
-        mul_x2(1, 0)
-        square_x2(1, 0)
+        weave_xp(0, 0)
+        make_diag(1)
+        make_d(0, 0)
+        make_d(1, 0)
+
+        tanh(1, 0)
+        tanh(1, 2)
+        scale_x(1, 0, nc.gpsimd)
+        turn_g(1, 0)
+        weave_g(1, 0, on_vector)
+        turn_g(1, 1)
+        weave_g(1, 1, on_vector)
+        square_tanh(1, 0, 0, H)
+        square_tanh(1, 2, 0, H)
+        dq_woven[0] = new_woven()
+        dq_woven[1] = new_woven()
+        weave_dq(0, 0)
+        quant_g(1)
+        mul_back(0, 1)
+        weave_dq(1, 0)
+        square_d2(0, 0)
+        make_d(0, 1)
         mul_back(1, 1)
-        make_e(1, 1)
-        mul_fish(0, 0, 0)
-        root(0, 0, 0)
-        mul_fish(0, 0, 3)
+        mul_x2(0, 1)
+        make_d(1, 1)
+        square_x2(0, 1)
+        quantize(x2, 0, x2_woven[0])
+        weave_dq(0, 1)
+        scale_x(1, 1, nc.gpsimd)
+        mul_x2(1, 0)
+        square_d2(0, 1)
+        quantize(d2, 0, d2_woven[0])
+        scale_x(1, 2, nc.gpsimd)
+        scale_x(1, 3, nc.gpsimd)
+        quantize(dq, 0, dq_woven[0])
+        weave_xp(0, 1)
+        xp_woven[1] = new_woven()
         mul_x2(1, 1)
+        square_x2(1, 0)
         square_x2(1, 1)
-        quant_dq(0)
-        mul_x2(2, 0)
-        mul_fish(0, 0, 1)
-        quant_xp(0)
-        mul_grad(0, 0, 3)
+        quantize(x2, 1, x2_woven[1])
+        quantize(xp, 0, xp_woven[0])
         weave_dq(1, 1)
-        mul_grad(0, 0, 1)
-        g_weave_dq(1, 0)
-        square_d(1, 1)
-        quant_d2(1)
-        root(0, 0, 3)
-        quant_x2(1)
-        quant_dq(1)
-        open_xp(2)
-        root(0, 0, 1)
-        half_finish(0, 0, 1)
-        divide(0, 0, 0)
-        mul_fish(0, 1, 0)
-        root(0, 1, 0)
-        square_x2(2, 0)
-        half_finish(0, 0, 3)
-        square_d(2, 0)
-        mul_grad(0, 0, 0)
-        finish(0, 0, 0)
-        weave_dq(2, 1)
-        rest_finish(0, 0, 3)
-        mul_grad(0, 1, 0)
-        square_d(2, 1)
-        rest_finish(0, 0, 1)
-        mul_fish(1, 1, 0)
-        root(1, 1, 0)
-        g_divide(0, 1, 0)
-        quant_d2(2)
-        g_finish(0, 1, 0)
-        mul_fish(1, 0, 0)
-        mul_grad(1, 0, 0)
-        root(1, 0, 0)
-        half_finish(1, 0, 0)
-        divide(1, 1, 0)
-        mul_grad(0, 1, 2)
-        mul_grad(1, 1, 0)
-        mul_fish(0, 1, 2)
-        root(0, 1, 2)
-        mul_x2(2, 1)
-        finish(1, 1, 0)
-        mul_fish(1, 0, 1)
-        g_weave_dq(2, 0)
-        half_finish(0, 1, 2)
-        rest_finish(1, 0, 0)
-        mul_fish(1, 2, 0)
-        rest_finish(0, 1, 2)
-        square_x2(2, 1)
-        quant_x2(2)
-        mul_fish(0, 2, 2)
-        root(1, 0, 1)
-        root(1, 2, 0)
-        quant_dq(2)
-        g_divide(1, 2, 0)
-        mul_grad(1, 0, 1)
-        divide(1, 0, 1)
-        finish(1, 0, 1)
-        mul_fish(0, 2, 0)
-        s_weave_xp(2, 1)
-        weave_xp(2, 0)
-        mul_fish(0, 0, 2)
-        root(0, 2, 0)
-        root(0, 2, 2)
-        root(0, 0, 2)
-        mul_fish(2, 1, 0)
-        mul_grad(0, 0, 2)
-        quant_xp(2)
-        mul_fish(2, 0, 1)
-        divide(0, 2, 2)
-        mul_grad(1, 2, 0)
-        g_finish(1, 2, 0)
-        divide(0, 0, 2)
-        mul_grad(0, 2, 2)
-        mul_grad(0, 2, 0)
-        g_divide(0, 2, 0)
-        mul_grad(2, 0, 1)
-        root(2, 1, 0)
-        root(2, 0, 1)
-        mul_grad(2, 1, 0)
-        g_divide(2, 0, 1)
-        finish(0, 2, 2)
-        mul_fish(2, 2, 0)
-        divide(2, 1, 0)
-        finish(0, 0, 2)
-        root(2, 2, 0)
-        mul_fish(2, 0, 0)
-        g_finish(0, 2, 0)
-        root(2, 0, 0)
-        finish(2, 1, 0)
-        mul_grad(2, 0, 0)
-        g_finish(2, 0, 1)
-        divide(2, 0, 0)
-        mul_grad(2, 2, 0)
-        finish(2, 0, 0)
-        g_divide(2, 2, 0)
-        g_finish(2, 2, 0)
+        square_d2(1, 0)
+        square_d2(1, 1)
+        quantize(d2, 1, d2_woven[1])
+
+        for k in range(len(tiles) + 1):
+            if k < len(tiles):
+                fish_bank[k] = product(k, x2, d2)
+            if k > 0:
+                grad_bank[k - 1] = product(k - 1, xp, dq)
+            if k < len(tiles):
+                inverse_root(k)
+            if k > 0:
+                finish(k - 1)
+            if k == 0:
+                quantize(dq, 1, dq_woven[1])
+                weave_xp(1, 0)
+            if k == 2:
+                weave_xp(1, 1)
+            if k == 4:
+                quantize(xp, 1, xp_woven[1])

@@ -5,6 +5,7 @@ from concourse.masks import make_identity
 
 N, D, H, O = 1024, 1024, 1024, 512
 FLOPS = 2 * N * H * O + 2 * 2 * N * D * H
+ROOT_N = 32.0
 DAMP = 0.2
 
 F32 = mybir.dt.float32
@@ -21,8 +22,11 @@ T = 4
 G = N // (P * T)
 HALF = 512
 M = HALF // P
+PAIR = 2 * P
 RUN = 4
+GAIN_COLS = 16
 TINY = 2.0**-100
+GPSIMD_FROM = 6
 
 
 def tile_diagonalfishernaturalgradient_kernel(tc, x, a, g, w2_bytes, w2_scale, p, q, s, out):
@@ -35,15 +39,8 @@ def tile_diagonalfishernaturalgradient_kernel(tc, x, a, g, w2_bytes, w2_scale, p
         def new_bank():
             return psum.tile([P, HALF], F32, name="bank")
 
-        gains = keep.tile([P, 3, 16], BF16, name="gains")
-        for n, vector in enumerate((p, q, s)):
-            nc.scalar.dma_start(
-                out=gains[:, n, 0 : G * T].rearrange("p (i t) -> p i t", t=T),
-                in_=vector.rearrange("(i p t) -> p i t", p=P, t=T),
-            )
+        gains = keep.tile([P, 3, GAIN_COLS], BF16, name="gains")
         w_scale = keep.tile([P, T], F32, name="w_scale")
-        nc.scalar.dma_start(out=w_scale[:], in_=w2_scale.rearrange("o (p t) -> p (o t)", t=T))
-
         w_bytes = [keep.tile([P, M * O], U8, name="w_bytes%d" % hh) for hh in range(2)]
         g_rows = [keep.tile([P, T, O], BF16, name="g_rows%d" % i) for i in range(G)]
         a_rows = [keep.tile([P, T, H], BF16, name="a_rows%d" % i) for i in range(G)]
@@ -51,24 +48,29 @@ def tile_diagonalfishernaturalgradient_kernel(tc, x, a, g, w2_bytes, w2_scale, p
 
         def load_w(hh):
             nc.sync.dma_start(
-                out=w_bytes[hh][:].rearrange("p (r k) -> p r k", k=O),
-                in_=w2_bytes.rearrange("(hh r p) k -> hh p r k", hh=2, p=P)[hh],
+                out=w_bytes[hh][:].rearrange("p (m k) -> p m k", k=O),
+                in_=w2_bytes.rearrange("(hh m p) k -> hh p m k", hh=2, p=P)[hh],
             )
 
-        def load(tiles, tensor, i, t0, t1):
+        def load_rows(tiles, tensor, i, t0, t1):
             rows = tensor.rearrange("(i p t) c -> i p t c", p=P, t=T)[i]
             nc.sync.dma_start(out=tiles[i][:, t0:t1], in_=rows[:, t0:t1])
 
         load_w(0)
         load_w(1)
-        load(a_rows, a, 0, 0, 2)
-        load(x_rows, x, 0, 0, 2)
-        load(a_rows, a, 0, 2, 4)
-        load(g_rows, g, 0, 0, 4)
-        load(x_rows, x, 0, 2, 4)
-        load(a_rows, a, 1, 0, 4)
-        load(g_rows, g, 1, 0, 4)
-        load(x_rows, x, 1, 0, 4)
+        nc.sync.dma_start(out=w_scale[:], in_=w2_scale.rearrange("o (p t) -> p (o t)", t=T))
+        for row, vector in enumerate((p, q, s)):
+            nc.sync.dma_start(
+                out=gains[:, row, 0 : G * T].rearrange("p (i t) -> p i t", t=T),
+                in_=vector.rearrange("(i p t) -> p i t", p=P, t=T),
+            )
+        load_rows(a_rows, a, 0, 0, 2)
+        load_rows(a_rows, a, 0, 2, 4)
+        load_rows(g_rows, g, 0, 0, 4)
+        load_rows(x_rows, x, 0, 0, 4)
+        load_rows(a_rows, a, 1, 0, 4)
+        load_rows(g_rows, g, 1, 0, 4)
+        load_rows(x_rows, x, 1, 0, 4)
 
         warm = keep.tile([P, 1], F32, name="warm")
         nc.vector.memset(warm[:], 0.0)
@@ -81,74 +83,87 @@ def tile_diagonalfishernaturalgradient_kernel(tc, x, a, g, w2_bytes, w2_scale, p
         quarter = keep.tile([P, 2, G * T], F32, name="quarter")
         nc.gpsimd.memset(quarter[:], 0.25)
         pqs = keep.tile([P, 3, G * T], F32, name="pqs")
-        nc.vector.tensor_copy(out=pqs[:], in_=gains[:, :, 0 : G * T])
         weight = keep.tile([P, 2, G * T], F32, name="weight")
-        nc.vector.tensor_tensor(out=weight[:], in0=pqs[:, 0:2, :], in1=pqs[:, 2:3, :].to_broadcast([P, 2, G * T]), op=ALU.mult)
         size = keep.tile([P, 2, G * T], F32, name="size")
-        nc.vector.scalar_tensor_tensor(out=size[:], in0=weight[:], scalar=-1.0, in1=weight[:], op0=ALU.mult, op1=ALU.max)
-        nc.vector.tensor_scalar(out=size[:], in0=size[:], scalar1=TINY, scalar2=None, op0=ALU.max)
         root4 = keep.tile([P, 2, G * T], F32, name="root4")
-        nc.gpsimd.tensor_tensor(
-            out=root4[:].rearrange("p a j -> p (a j)"), in0=size[:].rearrange("p a j -> p (a j)"),
-            in1=quarter[:].rearrange("p a j -> p (a j)"), op=ALU.pow,
-        )
         root2 = keep.tile([P, 2, G * T], F32, name="root2")
         r_head = keep.tile([P, G * T], BF16, name="r_head")
         r_tail = keep.tile([P, G * T], F32, name="r_tail")
         f_inverse = keep.tile([P, G * T], F32, name="f_inverse")
         ratio = keep.tile([P, G * T], F32, name="ratio")
 
-        def finish_factors():
+        def make_factors():
+            nc.vector.tensor_copy(out=pqs[:], in_=gains[:, :, 0 : G * T])
+            nc.vector.tensor_tensor(
+                out=weight[:], in0=pqs[:, 0:2, :], in1=pqs[:, 2:3, :].to_broadcast([P, 2, G * T]), op=ALU.mult
+            )
+            nc.vector.scalar_tensor_tensor(
+                out=size[:], in0=weight[:], scalar=-1.0, in1=weight[:], op0=ALU.mult, op1=ALU.max
+            )
+            nc.vector.tensor_scalar(out=size[:], in0=size[:], scalar1=TINY, scalar2=None, op0=ALU.max)
+            nc.gpsimd.tensor_tensor(
+                out=root4[:].rearrange("p v j -> p (v j)"),
+                in0=size[:].rearrange("p v j -> p (v j)"),
+                in1=quarter[:].rearrange("p v j -> p (v j)"),
+                op=ALU.pow,
+            )
             nc.gpsimd.tensor_tensor(out=root2[:], in0=root4[:], in1=root4[:], op=ALU.mult)
             nc.gpsimd.tensor_copy(out=r_head[:], in_=root2[:, 0, :])
             nc.gpsimd.tensor_tensor(out=r_tail[:], in0=root2[:, 0, :], in1=r_head[:], op=ALU.subtract)
+
+        def make_ratio():
             nc.vector.reciprocal(out=f_inverse[:], in_=root2[:, 1, :])
-            nc.vector.scalar_tensor_tensor(out=ratio[:], in0=f_inverse[:], scalar=-1.0, in1=pqs[:, 1, :], op0=ALU.mult, op1=ALU.mult)
+            nc.vector.scalar_tensor_tensor(
+                out=ratio[:], in0=f_inverse[:], scalar=-1.0, in1=pqs[:, 1, :], op0=ALU.mult, op1=ALU.mult
+            )
 
         diag = keep.tile([P, 2, G * T, P], BF16, name="diag")
 
         def make_diag(i):
             js = slice(i * T, (i + 1) * T)
-            for n, part in enumerate((root2[:, 0, js], r_tail[:, js])):
+            for part, factor in enumerate((root2[:, 0, js], r_tail[:, js])):
                 nc.gpsimd.tensor_tensor(
-                    out=diag[:, n, js, :], in0=ident_bf[:].unsqueeze(1).to_broadcast([P, T, P]),
-                    in1=part.unsqueeze(2).to_broadcast([P, T, P]), op=ALU.mult,
+                    out=diag[:, part, js, :],
+                    in0=ident_bf[:].unsqueeze(1).to_broadcast([P, T, P]),
+                    in1=factor.unsqueeze(2).to_broadcast([P, T, P]),
+                    op=ALU.mult,
                 )
 
-        def turn(bank, rows_bf16, col, stride):
-            words = rows_bf16.bitcast(F32)
+        def turn(bank, col, step, rows):
+            words = rows.bitcast(F32)
             for u in range(2):
-                nc.tensor.transpose(bank[:, col + u * stride : col + u * stride + P], words[:, u::2], ident[:])
+                nc.tensor.transpose(bank[:, col + u * step : col + u * step + P], words[:, u::2], ident[:])
 
         w_wide = [keep.tile([P, M * O], BF16, name="w_wide%d" % hh) for hh in range(2)]
         w_codes = keep.tile([P, H], U32, name="w_codes", align_bytes=64)
         w_scales = keep.tile([P, H], U8, name="w_scales", align_bytes=64)
-        scale_of_k = w_scale[:].rearrange("p (u e) -> p u e", e=2).unsqueeze(1).to_broadcast([P, 2 * P, 2, 2])
+        scale_of_k = w_scale[:].rearrange("p (u v) -> p u v", v=2).unsqueeze(1).to_broadcast([P, PAIR, 2, 2])
         w_banks, w_woven = {}, {}
 
-        def cast_w(hh, copy):
+        def widen_w(hh, copy):
             copy(out=w_wide[hh][:], in_=w_bytes[hh][:].bitcast(FP8))
 
         def turn_w(hh, b):
             w_banks[hh, b] = new_bank()
-            for n in range(2):
-                r = 2 * b + n
-                turn(w_banks[hh, b], w_wide[hh][:, r * O : (r + 1) * O], n * P, 2 * P)
+            for m in (2 * b, 2 * b + 1):
+                turn(w_banks[hh, b], (m - 2 * b) * P, PAIR, w_wide[hh][:, m * O : (m + 1) * O])
 
         def scale_w(hh, b):
             if b == 0:
                 w_woven[hh] = stage.tile([P, HALF, T], BF16, name="w_woven", tag="turned", bufs=3, align_bytes=64)
             nc.vector.tensor_tensor(
-                out=w_woven[hh][:, b * 2 * P : (b + 1) * 2 * P, :].rearrange("p h (u e) -> p h u e", e=2),
+                out=w_woven[hh][:, b * PAIR : (b + 1) * PAIR, :].rearrange("p h (u v) -> p h u v", v=2),
                 in0=scale_of_k,
-                in1=w_banks[hh, b][:].bitcast(BF16).rearrange("p (u h e) -> p h u e", u=2, e=2),
+                in1=w_banks[hh, b][:].bitcast(BF16).rearrange("p (u h v) -> p h u v", u=2, v=2),
                 op=ALU.mult,
             )
 
-        def quant_w(hh):
+        def quantize_w(hh):
             cols = slice(hh * HALF, (hh + 1) * HALF)
             nc.vector.quantize_mx(
-                out=w_codes[:, cols].bitcast(FP8X4), scales=w_scales[:, cols], in_=w_woven[hh][:].rearrange("p h t -> p (h t)")
+                out=w_codes[:, cols].bitcast(FP8X4),
+                scales=w_scales[:, cols],
+                in_=w_woven[hh][:].rearrange("p h t -> p (h t)"),
             )
 
         g_codes = keep.tile([P, G, HALF], U32, name="g_codes", align_bytes=64)
@@ -157,150 +172,184 @@ def tile_diagonalfishernaturalgradient_kernel(tc, x, a, g, w2_bytes, w2_scale, p
 
         def turn_g(i, b):
             g_banks[i, b] = new_bank()
-            for n in range(2):
-                turn(g_banks[i, b], g_rows[i][:, 2 * b + n, :], n * 2 * P, P)
+            for t in (2 * b, 2 * b + 1):
+                turn(g_banks[i, b], (t - 2 * b) * PAIR, P, g_rows[i][:, t, :])
 
         def weave_g(i, b, copy):
             if b == 0:
                 g_woven[i] = stage.tile([P, T * P, T], BF16, name="g_woven", tag="turned", bufs=3, align_bytes=64)
-            words = g_woven[i][:, b * 2 * P : (b + 1) * 2 * P, :].rearrange("p n t -> p (n t)").bitcast(F32)
+            words = g_woven[i][:, b * PAIR : (b + 1) * PAIR, :].rearrange("p c t -> p (c t)").bitcast(F32)
             copy(
-                out=words.rearrange("p (n m u) -> p n m u", n=2, u=2),
-                in_=g_banks[i, b][:].rearrange("p (n u m) -> p n m u", n=2, u=2),
+                out=words.rearrange("p (t m u) -> p t m u", t=2, u=2),
+                in_=g_banks[i, b][:].rearrange("p (t u m) -> p t m u", t=2, u=2),
             )
 
-        def quant_g(i):
+        def quantize_g(i):
             nc.vector.quantize_mx(
-                out=g_codes[:, i, :].bitcast(FP8X4), scales=g_scales[:, i, :], in_=g_woven[i][:].rearrange("p n t -> p (n t)")
+                out=g_codes[:, i, :].bitcast(FP8X4),
+                scales=g_scales[:, i, :],
+                in_=g_woven[i][:].rearrange("p c t -> p (c t)"),
             )
-
-        def code_tiles(name):
-            codes = [keep.tile([P, G, HALF], U32, name="%s_codes%d" % (name, n), align_bytes=64) for n in range(2)]
-            scales = [keep.tile([P, G, HALF], U8, name="%s_scales%d" % (name, n), align_bytes=64) for n in range(2)]
-            return codes, scales
 
         def new_woven():
             return stage.tile([P, G, HALF, T], BF16, name="woven", bufs=5, align_bytes=64)
 
-        def quantize(operand, n, woven):
-            codes, scales = operand
-            nc.vector.quantize_mx(
-                out=codes[n][:].rearrange("p i c -> p (i c)").bitcast(FP8X4),
-                scales=scales[n][:].rearrange("p i c -> p (i c)"),
-                in_=woven[:].rearrange("p i c t -> p (i c t)"),
-            )
-
-        def runs(planes):
-            return planes.rearrange("p t (c e) -> p c t e", e=RUN)
-
-        def woven_runs(woven, i):
-            return woven[:, i].rearrange("p (c e) t -> p c t e", e=RUN)
+        def code_tiles(name):
+            codes = [keep.tile([P, G, HALF], U32, name="%s_codes%d" % (name, half), align_bytes=64) for half in range(2)]
+            scales = [keep.tile([P, G, HALF], U8, name="%s_scales%d" % (name, half), align_bytes=64) for half in range(2)]
+            return codes, scales
 
         xp, x2, dq, d2 = code_tiles("xp"), code_tiles("x2"), code_tiles("dq"), code_tiles("d2")
+        xp_woven, x2_woven, dq_woven, d2_woven = {}, {}, {}, {}
+
+        def quantize(operand, woven, half):
+            codes, scales = operand
+            nc.vector.quantize_mx(
+                out=codes[half][:].rearrange("p i c -> p (i c)").bitcast(FP8X4),
+                scales=scales[half][:].rearrange("p i c -> p (i c)"),
+                in_=woven[half][:].rearrange("p i c t -> p (i c t)"),
+            )
+
+        def plane_runs(planes, half):
+            return planes[:, :, half * HALF : (half + 1) * HALF].rearrange("p t (c v) -> p c t v", v=RUN)
+
+        def woven_runs(woven, i):
+            return woven[:, i].rearrange("p (c v) t -> p c t v", v=RUN)
+
         xp_planes = [keep.tile([P, T, D], BF16, name="xp_planes%d" % i) for i in range(G)]
-        xp_woven, x2_woven, x2_banks = {}, {}, {}
 
         def scale_x(i, t, engine):
             gain = pqs[:, 0, i * T + t : i * T + t + 1]
-            engine.tensor_scalar(out=xp_planes[i][:, t, :], in0=x_rows[i][:, t, :], scalar1=gain, scalar2=0.0, op0=ALU.mult, op1=ALU.add)
+            engine.tensor_scalar(
+                out=xp_planes[i][:, t, :], in0=x_rows[i][:, t, :], scalar1=gain, scalar2=0.0, op0=ALU.mult, op1=ALU.add
+            )
 
-        def weave_xp(j, i):
-            nc.vector.tensor_copy(out=woven_runs(xp_woven[j], i), in_=runs(xp_planes[i][:, :, j * HALF : (j + 1) * HALF]))
+        def weave_xp(half, i):
+            nc.vector.tensor_copy(out=woven_runs(xp_woven[half], i), in_=plane_runs(xp_planes[i], half))
 
-        def mul_x2(j, i):
-            for b in range(M):
-                x2_banks[j, i, b] = new_bank()
-                cols = slice(j * HALF + b * P, j * HALF + (b + 1) * P)
+        x2_banks = {}
+
+        def mul_x2(half, i):
+            for m in range(M):
+                x2_banks[half, i, m] = new_bank()
+                cols = slice(half * HALF + m * P, half * HALF + (m + 1) * P)
                 for t in range(T):
-                    for n in range(2):
+                    for part in range(2):
                         nc.tensor.matmul(
-                            x2_banks[j, i, b][:, t * P : (t + 1) * P], lhsT=diag[:, n, i * T + t, :], rhs=x_rows[i][:, t, cols],
-                            start=(n == 0), stop=(n == 1),
+                            x2_banks[half, i, m][:, t * P : (t + 1) * P],
+                            lhsT=diag[:, part, i * T + t, :],
+                            rhs=x_rows[i][:, t, cols],
+                            start=(part == 0),
+                            stop=(part == 1),
                         )
 
-        def square_x2(j, i):
+        def square_x2(half, i):
             if i == 0:
-                x2_woven[j] = new_woven()
-            for b in range(M):
+                x2_woven[half] = new_woven()
+            for m in range(M):
                 nc.scalar.activation(
-                    out=x2_woven[j][:, i, b * P : (b + 1) * P, :], in_=x2_banks[j, i, b][:].rearrange("p (t c) -> p c t", t=T), func=ACT.Square
+                    out=x2_woven[half][:, i, m * P : (m + 1) * P, :],
+                    in_=x2_banks[half, i, m][:].rearrange("p (t c) -> p c t", t=T),
+                    func=ACT.Square,
                 )
 
         d_planes = [keep.tile([P, T, H], F32, name="d_planes%d" % i) for i in range(G)]
-        back_banks, dq_woven, d2_woven = {}, {}, {}
+        back_banks = {}
 
         def tanh(i, t0):
             nc.scalar.activation(out=d_planes[i][:, t0 : t0 + 2], in_=a_rows[i][:, t0 : t0 + 2], func=ACT.Tanh)
 
-        def square_tanh(i, t0, c0, c1):
-            for t in range(t0, t0 + 2):
-                plane = d_planes[i][:, t, c0:c1]
+        def square_tanh(i, t0):
+            for t in (t0, t0 + 1):
+                plane = d_planes[i][:, t, :]
                 nc.scalar.activation(out=plane, in_=plane, func=ACT.Square, scale=root4[:, 1, i * T + t : i * T + t + 1])
 
-        def mul_back(hh, i):
-            cols = slice(hh * HALF, (hh + 1) * HALF)
+        def mul_back(half, i):
+            cols = slice(half * HALF, (half + 1) * HALF)
             for t in range(T):
-                back_banks[hh, i, t] = new_bank()
+                back_banks[half, i, t] = new_bank()
                 rows = slice(t * P, (t + 1) * P)
                 nc.tensor.matmul_mx(
-                    out=back_banks[hh, i, t][:], lhsT=g_codes[:, i, rows].bitcast(FP8X4), lhsT_scale=g_scales[:, i, rows],
-                    rhs=w_codes[:, cols].bitcast(FP8X4), rhs_scale=w_scales[:, cols], start=True, stop=True,
+                    out=back_banks[half, i, t][:],
+                    lhsT=g_codes[:, i, rows].bitcast(FP8X4),
+                    lhsT_scale=g_scales[:, i, rows],
+                    rhs=w_codes[:, cols].bitcast(FP8X4),
+                    rhs_scale=w_scales[:, cols],
+                    start=True,
+                    stop=True,
                 )
 
-        def make_d(hh, i):
+        def make_d(half, i):
             for t in range(T):
-                plane = d_planes[i][:, t, hh * HALF : (hh + 1) * HALF]
-                f = root2[:, 1, i * T + t : i * T + t + 1]
-                nc.vector.scalar_tensor_tensor(out=plane, in0=plane, scalar=f, in1=back_banks[hh, i, t][:], op0=ALU.subtract, op1=ALU.mult)
+                plane = d_planes[i][:, t, half * HALF : (half + 1) * HALF]
+                nc.vector.scalar_tensor_tensor(
+                    out=plane,
+                    in0=plane,
+                    scalar=root2[:, 1, i * T + t : i * T + t + 1],
+                    in1=back_banks[half, i, t][:],
+                    op0=ALU.subtract,
+                    op1=ALU.mult,
+                )
 
-        def weave_dq(hh, i):
+        def weave_dq(half, i):
             factor = ratio[:, i * T : (i + 1) * T].unsqueeze(1).unsqueeze(3).to_broadcast([P, HALF // RUN, T, RUN])
             nc.vector.tensor_tensor(
-                out=woven_runs(dq_woven[hh], i), in0=runs(d_planes[i][:, :, hh * HALF : (hh + 1) * HALF]), in1=factor, op=ALU.mult
+                out=woven_runs(dq_woven[half], i), in0=plane_runs(d_planes[i], half), in1=factor, op=ALU.mult
             )
 
-        def square_d2(hh, i):
+        def square_d2(half, i):
             if i == 0:
-                d2_woven[hh] = new_woven()
-            nc.scalar.activation(out=woven_runs(d2_woven[hh], i), in_=runs(d_planes[i][:, :, hh * HALF : (hh + 1) * HALF]), func=ACT.Square)
+                d2_woven[half] = new_woven()
+            nc.scalar.activation(out=woven_runs(d2_woven[half], i), in_=plane_runs(d_planes[i], half), func=ACT.Square)
 
-        tiles = [(j, hh, m) for j in range(2) for hh in range(2) for m in range(M)]
-        fish_bank, grad_bank, root_of, inverse_of = {}, {}, {}, {}
+        tiles = [(xh, hh, m) for xh in range(2) for hh in range(2) for m in range(M)]
+        fisher_bank, grad_bank, root_of = {}, {}, {}
 
-        def product(k, lhs, rhs):
-            j, hh, m = tiles[k]
+        def product(number, left, right):
+            xh, hh, m = tiles[number]
             bank = new_bank()
             rows = slice(m * P, (m + 1) * P)
             for i in range(G):
                 nc.tensor.matmul_mx(
-                    out=bank[:], lhsT=lhs[0][j][:, i, rows].bitcast(FP8X4), lhsT_scale=lhs[1][j][:, i, rows],
-                    rhs=rhs[0][hh][:, i, :].bitcast(FP8X4), rhs_scale=rhs[1][hh][:, i, :], start=(i == 0), stop=(i == G - 1),
+                    out=bank[:],
+                    lhsT=left[0][xh][:, i, rows].bitcast(FP8X4),
+                    lhsT_scale=left[1][xh][:, i, rows],
+                    rhs=right[0][hh][:, i, :].bitcast(FP8X4),
+                    rhs_scale=right[1][hh][:, i, :],
+                    start=(i == 0),
+                    stop=(i == G - 1),
                 )
             return bank
 
-        def inverse_root(k):
-            root_of[k] = stage.tile([P, HALF], F32, name="root", bufs=4)
-            nc.scalar.activation(out=root_of[k][:], in_=fish_bank[k][:], func=ACT.Abs_reciprocal_sqrt, scale=1.0 / 32.0, bias=32.0 * DAMP)
+        def inverse_root(number):
+            root_of[number] = stage.tile([P, HALF], F32, name="root", bufs=4)
+            nc.scalar.activation(
+                out=root_of[number][:],
+                in_=fisher_bank[number][:],
+                func=ACT.Abs_reciprocal_sqrt,
+                scale=1.0 / ROOT_N,
+                bias=ROOT_N * DAMP,
+            )
 
-        def finish(k):
-            j, hh, m = tiles[k]
-            if k > 5 and k % 2 == 1:
+        def finish(number):
+            if number >= GPSIMD_FROM and number % 2 == 1:
                 inverse = stage.tile([P, HALF], F32, name="inverse_g")
-                nc.gpsimd.tensor_tensor(out=inverse[:], in0=root_of[k][:], in1=root_of[k][:], op=ALU.mult)
+                nc.gpsimd.tensor_tensor(out=inverse[:], in0=root_of[number][:], in1=root_of[number][:], op=ALU.mult)
             else:
                 inverse = stage.tile([P, HALF], F32, name="inverse_s")
-                nc.scalar.activation(out=inverse[:], in_=root_of[k][:], func=ACT.Square)
+                nc.scalar.activation(out=inverse[:], in_=root_of[number][:], func=ACT.Square)
             result = stage.tile([P, HALF], F32, name="result", bufs=4)
-            nc.vector.tensor_tensor(out=result[:], in0=inverse[:], in1=grad_bank[k][:], op=ALU.mult)
-            row = j * HALF + m * P
+            nc.vector.tensor_tensor(out=result[:], in0=inverse[:], in1=grad_bank[number][:], op=ALU.mult)
+            xh, hh, m = tiles[number]
+            row = xh * HALF + m * P
             nc.sync.dma_start(out=out[row : row + P, hh * HALF : (hh + 1) * HALF], in_=result[:])
 
         ctx.enter_context(tc.manual_schedule())
         on_scalar, on_vector = nc.scalar.copy, nc.vector.tensor_copy
 
-        cast_w(0, on_scalar)
-        cast_w(1, on_vector)
-        finish_factors()
+        widen_w(0, on_scalar)
+        widen_w(1, on_vector)
+        make_factors()
         xp_woven[0] = new_woven()
         turn_w(0, 0)
         scale_w(0, 0)
@@ -314,20 +363,19 @@ def tile_diagonalfishernaturalgradient_kernel(tc, x, a, g, w2_bytes, w2_scale, p
         turn_w(1, 1)
         for t in range(T):
             scale_x(0, t, nc.vector)
-        square_tanh(0, 0, 0, HALF)
-        quant_w(0)
+        square_tanh(0, 0)
+        quantize_w(0)
         turn_g(0, 0)
         turn_g(0, 1)
         weave_g(0, 0, on_vector)
         weave_g(0, 1, on_scalar)
-        square_tanh(0, 2, 0, HALF)
-        square_tanh(0, 0, HALF, H)
+        square_tanh(0, 2)
         mul_x2(0, 0)
         scale_w(1, 1)
-        quant_g(0)
-        quant_w(1)
+        quantize_g(0)
+        quantize_w(1)
+        make_ratio()
         square_x2(0, 0)
-        square_tanh(0, 2, HALF, H)
         mul_back(0, 0)
         mul_back(1, 0)
         weave_xp(0, 0)
@@ -339,15 +387,15 @@ def tile_diagonalfishernaturalgradient_kernel(tc, x, a, g, w2_bytes, w2_scale, p
         tanh(1, 2)
         scale_x(1, 0, nc.gpsimd)
         turn_g(1, 0)
-        weave_g(1, 0, on_vector)
+        weave_g(1, 0, on_scalar)
         turn_g(1, 1)
         weave_g(1, 1, on_vector)
-        square_tanh(1, 0, 0, H)
-        square_tanh(1, 2, 0, H)
+        square_tanh(1, 0)
+        square_tanh(1, 2)
         dq_woven[0] = new_woven()
         dq_woven[1] = new_woven()
         weave_dq(0, 0)
-        quant_g(1)
+        quantize_g(1)
         mul_back(0, 1)
         weave_dq(1, 0)
         square_d2(0, 0)
@@ -356,40 +404,41 @@ def tile_diagonalfishernaturalgradient_kernel(tc, x, a, g, w2_bytes, w2_scale, p
         mul_x2(0, 1)
         make_d(1, 1)
         square_x2(0, 1)
-        quantize(x2, 0, x2_woven[0])
+        quantize(x2, x2_woven, 0)
         weave_dq(0, 1)
         scale_x(1, 1, nc.gpsimd)
         mul_x2(1, 0)
         square_d2(0, 1)
-        quantize(d2, 0, d2_woven[0])
+        quantize(d2, d2_woven, 0)
         scale_x(1, 2, nc.gpsimd)
         scale_x(1, 3, nc.gpsimd)
-        quantize(dq, 0, dq_woven[0])
+        quantize(dq, dq_woven, 0)
         weave_xp(0, 1)
         xp_woven[1] = new_woven()
         mul_x2(1, 1)
         square_x2(1, 0)
         square_x2(1, 1)
-        quantize(x2, 1, x2_woven[1])
-        quantize(xp, 0, xp_woven[0])
+        quantize(x2, x2_woven, 1)
+        quantize(xp, xp_woven, 0)
         weave_dq(1, 1)
         square_d2(1, 0)
         square_d2(1, 1)
-        quantize(d2, 1, d2_woven[1])
+        quantize(d2, d2_woven, 1)
 
-        for k in range(len(tiles) + 1):
-            if k < len(tiles):
-                fish_bank[k] = product(k, x2, d2)
-            if k > 0:
-                grad_bank[k - 1] = product(k - 1, xp, dq)
-            if k < len(tiles):
-                inverse_root(k)
-            if k > 0:
-                finish(k - 1)
-            if k == 0:
-                quantize(dq, 1, dq_woven[1])
+        for turn_number in range(len(tiles) + 1):
+            opened, closed = turn_number, turn_number - 1
+            if opened < len(tiles):
+                fisher_bank[opened] = product(opened, x2, d2)
+            if closed >= 0:
+                grad_bank[closed] = product(closed, xp, dq)
+            if opened < len(tiles):
+                inverse_root(opened)
+            if closed >= 0:
+                finish(closed)
+            if turn_number == 0:
+                quantize(dq, dq_woven, 1)
                 weave_xp(1, 0)
-            if k == 2:
+            if turn_number == 2:
                 weave_xp(1, 1)
-            if k == 4:
-                quantize(xp, 1, xp_woven[1])
+            if turn_number == 4:
+                quantize(xp, xp_woven, 1)

from contextlib import ExitStack

import concourse.mybir as mybir
from concourse.masks import make_identity

N, D, H, O = 1024, 1024, 1024, 512
FLOPS = 2 * N * H * O + 2 * 2 * N * D * H
ROOT_N = 32.0
DAMP = 0.2

F32 = mybir.dt.float32
BF16 = mybir.dt.bfloat16
U32 = mybir.dt.uint32
U8 = mybir.dt.uint8
FP8 = mybir.dt.float8_e4m3fn
FP8X4 = mybir.dt.float8_e4m3fn_x4
ALU = mybir.AluOpType
ACT = mybir.ActivationFunctionType

P = 128
T = 4
G = N // (P * T)
HALF = 512
M = HALF // P
PAIR = 2 * P
RUN = 4
GAIN_COLS = 16
TINY = 2.0**-100
GPSIMD_FROM = 6


def tile_diagonalfishernaturalgradient_kernel(tc, x, a, g, w2_bytes, w2_scale, p, q, s, out):
    nc = tc.nc
    with ExitStack() as ctx:
        keep = ctx.enter_context(tc.tile_pool(name="keep", bufs=1))
        stage = ctx.enter_context(tc.tile_pool(name="stage", bufs=2))
        psum = ctx.enter_context(tc.psum_pool(name="psum", bufs=8))

        def new_bank():
            return psum.tile([P, HALF], F32, name="bank")

        gains = keep.tile([P, 3, GAIN_COLS], BF16, name="gains")
        w_scale = keep.tile([P, T], F32, name="w_scale")
        w_bytes = [keep.tile([P, M * O], U8, name="w_bytes%d" % hh) for hh in range(2)]
        g_rows = [keep.tile([P, T, O], BF16, name="g_rows%d" % i) for i in range(G)]
        a_rows = [keep.tile([P, T, H], BF16, name="a_rows%d" % i) for i in range(G)]
        x_rows = [keep.tile([P, T, D], BF16, name="x_rows%d" % i) for i in range(G)]

        def load_w(hh):
            nc.sync.dma_start(
                out=w_bytes[hh][:].rearrange("p (m k) -> p m k", k=O),
                in_=w2_bytes.rearrange("(hh m p) k -> hh p m k", hh=2, p=P)[hh],
            )

        def load_rows(tiles, tensor, i, t0, t1):
            rows = tensor.rearrange("(i p t) c -> i p t c", p=P, t=T)[i]
            nc.sync.dma_start(out=tiles[i][:, t0:t1], in_=rows[:, t0:t1])

        load_w(0)
        load_w(1)
        nc.sync.dma_start(out=w_scale[:], in_=w2_scale.rearrange("o (p t) -> p (o t)", t=T))
        for row, vector in enumerate((p, q, s)):
            nc.sync.dma_start(
                out=gains[:, row, 0 : G * T].rearrange("p (i t) -> p i t", t=T),
                in_=vector.rearrange("(i p t) -> p i t", p=P, t=T),
            )
        load_rows(a_rows, a, 0, 0, 2)
        load_rows(a_rows, a, 0, 2, 4)
        load_rows(g_rows, g, 0, 0, 4)
        load_rows(x_rows, x, 0, 0, 4)
        load_rows(a_rows, a, 1, 0, 4)
        load_rows(g_rows, g, 1, 0, 4)
        load_rows(x_rows, x, 1, 0, 4)

        warm = keep.tile([P, 1], F32, name="warm")
        nc.vector.memset(warm[:], 0.0)
        nc.scalar.activation(out=warm[:], in_=warm[:], func=ACT.Tanh)
        ident = keep.tile([P, P], F32, name="ident")
        make_identity(nc, ident[:])
        ident_bf = keep.tile([P, P], BF16, name="ident_bf")
        nc.vector.tensor_copy(out=ident_bf[:], in_=ident[:])

        quarter = keep.tile([P, 2, G * T], F32, name="quarter")
        nc.gpsimd.memset(quarter[:], 0.25)
        pqs = keep.tile([P, 3, G * T], F32, name="pqs")
        weight = keep.tile([P, 2, G * T], F32, name="weight")
        size = keep.tile([P, 2, G * T], F32, name="size")
        root4 = keep.tile([P, 2, G * T], F32, name="root4")
        root2 = keep.tile([P, 2, G * T], F32, name="root2")
        r_head = keep.tile([P, G * T], BF16, name="r_head")
        r_tail = keep.tile([P, G * T], F32, name="r_tail")
        f_inverse = keep.tile([P, G * T], F32, name="f_inverse")
        ratio = keep.tile([P, G * T], F32, name="ratio")

        def make_factors():
            nc.vector.tensor_copy(out=pqs[:], in_=gains[:, :, 0 : G * T])
            nc.vector.tensor_tensor(
                out=weight[:], in0=pqs[:, 0:2, :], in1=pqs[:, 2:3, :].to_broadcast([P, 2, G * T]), op=ALU.mult
            )
            nc.vector.scalar_tensor_tensor(
                out=size[:], in0=weight[:], scalar=-1.0, in1=weight[:], op0=ALU.mult, op1=ALU.max
            )
            nc.vector.tensor_scalar(out=size[:], in0=size[:], scalar1=TINY, scalar2=None, op0=ALU.max)
            nc.gpsimd.tensor_tensor(
                out=root4[:].rearrange("p v j -> p (v j)"),
                in0=size[:].rearrange("p v j -> p (v j)"),
                in1=quarter[:].rearrange("p v j -> p (v j)"),
                op=ALU.pow,
            )
            nc.gpsimd.tensor_tensor(out=root2[:], in0=root4[:], in1=root4[:], op=ALU.mult)
            nc.gpsimd.tensor_copy(out=r_head[:], in_=root2[:, 0, :])
            nc.gpsimd.tensor_tensor(out=r_tail[:], in0=root2[:, 0, :], in1=r_head[:], op=ALU.subtract)

        def make_ratio():
            nc.vector.reciprocal(out=f_inverse[:], in_=root2[:, 1, :])
            nc.vector.scalar_tensor_tensor(
                out=ratio[:], in0=f_inverse[:], scalar=-1.0, in1=pqs[:, 1, :], op0=ALU.mult, op1=ALU.mult
            )

        diag = keep.tile([P, 2, G * T, P], BF16, name="diag")

        def make_diag(i):
            js = slice(i * T, (i + 1) * T)
            for part, factor in enumerate((root2[:, 0, js], r_tail[:, js])):
                nc.gpsimd.tensor_tensor(
                    out=diag[:, part, js, :],
                    in0=ident_bf[:].unsqueeze(1).to_broadcast([P, T, P]),
                    in1=factor.unsqueeze(2).to_broadcast([P, T, P]),
                    op=ALU.mult,
                )

        def turn(bank, col, step, rows):
            words = rows.bitcast(F32)
            for u in range(2):
                nc.tensor.transpose(bank[:, col + u * step : col + u * step + P], words[:, u::2], ident[:])

        w_wide = [keep.tile([P, M * O], BF16, name="w_wide%d" % hh) for hh in range(2)]
        w_codes = keep.tile([P, H], U32, name="w_codes", align_bytes=64)
        w_scales = keep.tile([P, H], U8, name="w_scales", align_bytes=64)
        scale_of_k = w_scale[:].rearrange("p (u v) -> p u v", v=2).unsqueeze(1).to_broadcast([P, PAIR, 2, 2])
        w_banks, w_woven = {}, {}

        def widen_w(hh, copy):
            copy(out=w_wide[hh][:], in_=w_bytes[hh][:].bitcast(FP8))

        def turn_w(hh, b):
            w_banks[hh, b] = new_bank()
            for m in (2 * b, 2 * b + 1):
                turn(w_banks[hh, b], (m - 2 * b) * P, PAIR, w_wide[hh][:, m * O : (m + 1) * O])

        def scale_w(hh, b):
            if b == 0:
                w_woven[hh] = stage.tile([P, HALF, T], BF16, name="w_woven", tag="turned", bufs=3, align_bytes=64)
            nc.vector.tensor_tensor(
                out=w_woven[hh][:, b * PAIR : (b + 1) * PAIR, :].rearrange("p h (u v) -> p h u v", v=2),
                in0=scale_of_k,
                in1=w_banks[hh, b][:].bitcast(BF16).rearrange("p (u h v) -> p h u v", u=2, v=2),
                op=ALU.mult,
            )

        def quantize_w(hh):
            cols = slice(hh * HALF, (hh + 1) * HALF)
            nc.vector.quantize_mx(
                out=w_codes[:, cols].bitcast(FP8X4),
                scales=w_scales[:, cols],
                in_=w_woven[hh][:].rearrange("p h t -> p (h t)"),
            )

        g_codes = keep.tile([P, G, HALF], U32, name="g_codes", align_bytes=64)
        g_scales = keep.tile([P, G, HALF], U8, name="g_scales", align_bytes=64)
        g_banks, g_woven = {}, {}

        def turn_g(i, b):
            g_banks[i, b] = new_bank()
            for t in (2 * b, 2 * b + 1):
                turn(g_banks[i, b], (t - 2 * b) * PAIR, P, g_rows[i][:, t, :])

        def weave_g(i, b, copy):
            if b == 0:
                g_woven[i] = stage.tile([P, T * P, T], BF16, name="g_woven", tag="turned", bufs=3, align_bytes=64)
            words = g_woven[i][:, b * PAIR : (b + 1) * PAIR, :].rearrange("p c t -> p (c t)").bitcast(F32)
            copy(
                out=words.rearrange("p (t m u) -> p t m u", t=2, u=2),
                in_=g_banks[i, b][:].rearrange("p (t u m) -> p t m u", t=2, u=2),
            )

        def quantize_g(i):
            nc.vector.quantize_mx(
                out=g_codes[:, i, :].bitcast(FP8X4),
                scales=g_scales[:, i, :],
                in_=g_woven[i][:].rearrange("p c t -> p (c t)"),
            )

        def new_woven():
            return stage.tile([P, G, HALF, T], BF16, name="woven", bufs=5, align_bytes=64)

        def code_tiles(name):
            codes = [keep.tile([P, G, HALF], U32, name="%s_codes%d" % (name, half), align_bytes=64) for half in range(2)]
            scales = [keep.tile([P, G, HALF], U8, name="%s_scales%d" % (name, half), align_bytes=64) for half in range(2)]
            return codes, scales

        xp, x2, dq, d2 = code_tiles("xp"), code_tiles("x2"), code_tiles("dq"), code_tiles("d2")
        xp_woven, x2_woven, dq_woven, d2_woven = {}, {}, {}, {}

        def quantize(operand, woven, half):
            codes, scales = operand
            nc.vector.quantize_mx(
                out=codes[half][:].rearrange("p i c -> p (i c)").bitcast(FP8X4),
                scales=scales[half][:].rearrange("p i c -> p (i c)"),
                in_=woven[half][:].rearrange("p i c t -> p (i c t)"),
            )

        def plane_runs(planes, half):
            return planes[:, :, half * HALF : (half + 1) * HALF].rearrange("p t (c v) -> p c t v", v=RUN)

        def woven_runs(woven, i):
            return woven[:, i].rearrange("p (c v) t -> p c t v", v=RUN)

        xp_planes = [keep.tile([P, T, D], BF16, name="xp_planes%d" % i) for i in range(G)]

        def scale_x(i, t, engine):
            gain = pqs[:, 0, i * T + t : i * T + t + 1]
            engine.tensor_scalar(
                out=xp_planes[i][:, t, :], in0=x_rows[i][:, t, :], scalar1=gain, scalar2=0.0, op0=ALU.mult, op1=ALU.add
            )

        def weave_xp(half, i):
            nc.vector.tensor_copy(out=woven_runs(xp_woven[half], i), in_=plane_runs(xp_planes[i], half))

        x2_banks = {}

        def mul_x2(half, i):
            for m in range(M):
                x2_banks[half, i, m] = new_bank()
                cols = slice(half * HALF + m * P, half * HALF + (m + 1) * P)
                for t in range(T):
                    for part in range(2):
                        nc.tensor.matmul(
                            x2_banks[half, i, m][:, t * P : (t + 1) * P],
                            lhsT=diag[:, part, i * T + t, :],
                            rhs=x_rows[i][:, t, cols],
                            start=(part == 0),
                            stop=(part == 1),
                        )

        def square_x2(half, i):
            if i == 0:
                x2_woven[half] = new_woven()
            for m in range(M):
                nc.scalar.activation(
                    out=x2_woven[half][:, i, m * P : (m + 1) * P, :],
                    in_=x2_banks[half, i, m][:].rearrange("p (t c) -> p c t", t=T),
                    func=ACT.Square,
                )

        d_planes = [keep.tile([P, T, H], F32, name="d_planes%d" % i) for i in range(G)]
        back_banks = {}

        def tanh(i, t0):
            nc.scalar.activation(out=d_planes[i][:, t0 : t0 + 2], in_=a_rows[i][:, t0 : t0 + 2], func=ACT.Tanh)

        def square_tanh(i, t0):
            for t in (t0, t0 + 1):
                plane = d_planes[i][:, t, :]
                nc.scalar.activation(out=plane, in_=plane, func=ACT.Square, scale=root4[:, 1, i * T + t : i * T + t + 1])

        def mul_back(half, i):
            cols = slice(half * HALF, (half + 1) * HALF)
            for t in range(T):
                back_banks[half, i, t] = new_bank()
                rows = slice(t * P, (t + 1) * P)
                nc.tensor.matmul_mx(
                    out=back_banks[half, i, t][:],
                    lhsT=g_codes[:, i, rows].bitcast(FP8X4),
                    lhsT_scale=g_scales[:, i, rows],
                    rhs=w_codes[:, cols].bitcast(FP8X4),
                    rhs_scale=w_scales[:, cols],
                    start=True,
                    stop=True,
                )

        def make_d(half, i):
            for t in range(T):
                plane = d_planes[i][:, t, half * HALF : (half + 1) * HALF]
                nc.vector.scalar_tensor_tensor(
                    out=plane,
                    in0=plane,
                    scalar=root2[:, 1, i * T + t : i * T + t + 1],
                    in1=back_banks[half, i, t][:],
                    op0=ALU.subtract,
                    op1=ALU.mult,
                )

        def weave_dq(half, i):
            factor = ratio[:, i * T : (i + 1) * T].unsqueeze(1).unsqueeze(3).to_broadcast([P, HALF // RUN, T, RUN])
            nc.vector.tensor_tensor(
                out=woven_runs(dq_woven[half], i), in0=plane_runs(d_planes[i], half), in1=factor, op=ALU.mult
            )

        def square_d2(half, i):
            if i == 0:
                d2_woven[half] = new_woven()
            nc.scalar.activation(out=woven_runs(d2_woven[half], i), in_=plane_runs(d_planes[i], half), func=ACT.Square)

        tiles = [(xh, hh, m) for xh in range(2) for hh in range(2) for m in range(M)]
        fisher_bank, grad_bank, root_of = {}, {}, {}

        def product(number, left, right):
            xh, hh, m = tiles[number]
            bank = new_bank()
            rows = slice(m * P, (m + 1) * P)
            for i in range(G):
                nc.tensor.matmul_mx(
                    out=bank[:],
                    lhsT=left[0][xh][:, i, rows].bitcast(FP8X4),
                    lhsT_scale=left[1][xh][:, i, rows],
                    rhs=right[0][hh][:, i, :].bitcast(FP8X4),
                    rhs_scale=right[1][hh][:, i, :],
                    start=(i == 0),
                    stop=(i == G - 1),
                )
            return bank

        def inverse_root(number):
            root_of[number] = stage.tile([P, HALF], F32, name="root", bufs=4)
            nc.scalar.activation(
                out=root_of[number][:],
                in_=fisher_bank[number][:],
                func=ACT.Abs_reciprocal_sqrt,
                scale=1.0 / ROOT_N,
                bias=ROOT_N * DAMP,
            )

        def finish(number):
            if number >= GPSIMD_FROM and number % 2 == 1:
                inverse = stage.tile([P, HALF], F32, name="inverse_g")
                nc.gpsimd.tensor_tensor(out=inverse[:], in0=root_of[number][:], in1=root_of[number][:], op=ALU.mult)
            else:
                inverse = stage.tile([P, HALF], F32, name="inverse_s")
                nc.scalar.activation(out=inverse[:], in_=root_of[number][:], func=ACT.Square)
            result = stage.tile([P, HALF], F32, name="result", bufs=4)
            nc.vector.tensor_tensor(out=result[:], in0=inverse[:], in1=grad_bank[number][:], op=ALU.mult)
            xh, hh, m = tiles[number]
            row = xh * HALF + m * P
            nc.sync.dma_start(out=out[row : row + P, hh * HALF : (hh + 1) * HALF], in_=result[:])

        ctx.enter_context(tc.manual_schedule())
        on_scalar, on_vector = nc.scalar.copy, nc.vector.tensor_copy

        widen_w(0, on_scalar)
        widen_w(1, on_vector)
        make_factors()
        xp_woven[0] = new_woven()
        turn_w(0, 0)
        scale_w(0, 0)
        make_diag(0)
        turn_w(0, 1)
        scale_w(0, 1)
        tanh(0, 0)
        turn_w(1, 0)
        scale_w(1, 0)
        tanh(0, 2)
        turn_w(1, 1)
        for t in range(T):
            scale_x(0, t, nc.vector)
        square_tanh(0, 0)
        quantize_w(0)
        turn_g(0, 0)
        turn_g(0, 1)
        weave_g(0, 0, on_vector)
        weave_g(0, 1, on_scalar)
        square_tanh(0, 2)
        mul_x2(0, 0)
        scale_w(1, 1)
        quantize_g(0)
        quantize_w(1)
        make_ratio()
        square_x2(0, 0)
        mul_back(0, 0)
        mul_back(1, 0)
        weave_xp(0, 0)
        make_diag(1)
        make_d(0, 0)
        make_d(1, 0)

        tanh(1, 0)
        tanh(1, 2)
        scale_x(1, 0, nc.gpsimd)
        turn_g(1, 0)
        weave_g(1, 0, on_scalar)
        turn_g(1, 1)
        weave_g(1, 1, on_vector)
        square_tanh(1, 0)
        square_tanh(1, 2)
        dq_woven[0] = new_woven()
        dq_woven[1] = new_woven()
        weave_dq(0, 0)
        quantize_g(1)
        mul_back(0, 1)
        weave_dq(1, 0)
        square_d2(0, 0)
        make_d(0, 1)
        mul_back(1, 1)
        mul_x2(0, 1)
        make_d(1, 1)
        square_x2(0, 1)
        quantize(x2, x2_woven, 0)
        weave_dq(0, 1)
        scale_x(1, 1, nc.gpsimd)
        mul_x2(1, 0)
        square_d2(0, 1)
        quantize(d2, d2_woven, 0)
        scale_x(1, 2, nc.gpsimd)
        scale_x(1, 3, nc.gpsimd)
        quantize(dq, dq_woven, 0)
        weave_xp(0, 1)
        xp_woven[1] = new_woven()
        mul_x2(1, 1)
        square_x2(1, 0)
        square_x2(1, 1)
        quantize(x2, x2_woven, 1)
        quantize(xp, xp_woven, 0)
        weave_dq(1, 1)
        square_d2(1, 0)
        square_d2(1, 1)
        quantize(d2, d2_woven, 1)

        for turn_number in range(len(tiles) + 1):
            opened, closed = turn_number, turn_number - 1
            if opened < len(tiles):
                fisher_bank[opened] = product(opened, x2, d2)
            if closed >= 0:
                grad_bank[closed] = product(closed, xp, dq)
            if opened < len(tiles):
                inverse_root(opened)
            if closed >= 0:
                finish(closed)
            if turn_number == 0:
                quantize(dq, dq_woven, 1)
                weave_xp(1, 0)
            if turn_number == 2:
                weave_xp(1, 1)
            if turn_number == 4:
                quantize(xp, xp_woven, 1)
